import numpy as np, ml_dtypes
CORES = [10,34,74,98]
N = 4
import mx_ref
BF = ml_dtypes.bfloat16
def gcols(t, e):
    v = np.concatenate([t.reshape(8, 16, -1, 4), np.zeros((8, 16, 1, 4), BF)], axis=2)
    return np.ascontiguousarray(np.stack([v[g][:, e[g]] for g in range(8)])).reshape(128, -1)
def tile(rs):
    return np.stack(rs, axis=2).reshape(128, -1).astype(BF)
def pick(q, e):
    c = np.concatenate([q[0].reshape(128, -1, 4), np.zeros((128, 1, 4), np.uint8)], axis=1); s = np.concatenate([q[1], np.ones((16, 1), np.uint8)], axis=1)
    return (np.ascontiguousarray(c[:, e].reshape(128, -1)), np.ascontiguousarray(s[:, e]))
def join(*qs):
    return (np.concatenate([q[0] for q in qs], axis=1), np.concatenate([q[1] for q in qs], axis=1))
def put(q, e, v):
    c, s = q[0].reshape(128, -1, 4).copy(), q[1].copy(); c[:, e] = v[0].reshape(128, -1, 4); s[:, e] = v[1]
    return (c.reshape(128, -1), s)
def pk(c, s):
    return (np.ascontiguousarray(c), mx_ref.live(s))
def emit(q):
    return q[0], q[1]
def packed(v, rng):
    q = [mx_ref.quantize(np.ascontiguousarray(v[r])) for r in range(N)]
    return np.stack([a for a, b in q]), np.stack([mx_ref.plane(b, rng) for a, b in q])
def values_of_codes():
    e, c = np.zeros((128, 128, 4), np.float32), np.zeros((128, 2, 4), np.uint8)
    e[np.arange(128), np.arange(128), 0] = 1
    c[:127, :, 0] = np.arange(256).reshape(2, 128).T[:127]
    return mx_ref.matmul(mx_ref.quantize(e.reshape(128, 512).astype(BF)), (c.reshape(128, 8), np.full((16, 2), 127, np.uint8))).T.reshape(-1).astype(np.float64)
CODE_VALUE, SCALE_VALUE = values_of_codes(), 2.0 ** (np.arange(256) - 127.0)
def decode(q):
    return (CODE_VALUE[q[0]].reshape(16, 8, -1, 4) * SCALE_VALUE[q[1]][:, None, :, None] + 0.0).reshape(128, -1).astype(np.float32)
def f(rng, *shape):
    return mx_ref.flush((rng.standard_normal(shape, dtype=np.float32) * np.exp2(rng.integers(-2, 3, shape[:-1] + (1,)))).astype(BF))
def wide(rng, *shape, cols=0):
    v = rng.standard_normal(shape, dtype=np.float32) * np.exp2(rng.integers(-12, 13, shape)).astype(np.float32)
    if cols: v *= np.repeat(np.exp2(rng.integers(-cols, cols + 1, shape[:-2] + (1, shape[-1] // 4))) * (rng.random(shape[:-2] + (1, shape[-1] // 4)) > 0.0625), 4, axis=-1).astype(np.float32)
    return mx_ref.flush(v.astype(BF))
C, K, LB = 224, 48, 6
def layer(w, g, t):
    return tile([mx_ref.matmul(pick(w, np.arange(128 * b, 128 * b + 128)), g) * np.float32(0.015625) + t[:, b::4] for b in range(4)])
def numbers_of(rng):
    return {"x": np.array(f(rng, N, 128, 4 * C)), "q": np.array(f(rng, N, 128, 4 * K)), "u": np.array(f(rng, N, 128, 512)), "z": np.array(f(rng, N, 128, 512)), "v": np.array(f(rng, N, 128, 512))}
def weights(rng, w):
    c, p = packed(w, rng)
    return {"wc": c, "ws": p}
def still(rng, k):
    w = np.zeros((N, 128, 4, 128, 4), np.float32)
    i = np.arange(128)
    for b in range(4): w[:, i, b, i, b] = k
    return weights(rng, w.reshape(N, 128, 2048).astype(BF))
def marked(rng, s, size):
    d = numbers_of(rng)
    c = size[:, None, None, None, None]
    m = rng.choice([-1.0, 0.0, 1.0], (N, 8, 8, C, 4))
    m[:, :, :4, :, 0] = 1.125 * s
    m[:, :, 4:, :, 0] = s
    m[..., 3] = 0
    d["x"].reshape(N, 8, 16, C, 4)[:, :, :8] = (m * c).astype(np.float32).astype(BF)
    h = rng.choice([1.0, 1.0, -1.0, 0.0], (N, 8, LB + 7, K))
    h[..., 0] = -1
    h[..., 1] = 1
    h[:, :, :LB, 2] = 1
    h[:, :, LB:, 2] = -1
    h[:, :, :LB, 3] = -1
    h[:, :, LB:, 3] = 1
    h[..., 4] = 0
    m = rng.choice([-1.0, 0.0, 1.0], (N, 8, 16, K, 4))
    m[:, :, :LB + 7, :, 3] = 1.125 * h
    m[..., 0][:, :, (np.arange(LB + 7) + 8) % 16] = h
    d["q"] = (m * c).astype(np.float32).astype(BF).reshape(N, 128, 4 * K)
    u, z = d["u"].reshape(N, 8, 16, 128, 4), d["z"].reshape(N, 8, 16, 128, 4)
    u[:, :, :, ::16] = 0
    z[:, :, :, np.arange(128) % 16 < LB + 7] = 0
    i = np.arange(N)
    plus, minus = (1.125 * size).astype(np.float32).astype(BF), (-1.25 * size).astype(np.float32).astype(BF)
    for g in range(8):
        u[i, g, i % 4, 16 * g, 0] = plus
        u[i, g, 4 + i % 4, 16 * g, 0] = minus
        for e in range(LB + 7):
            z[i, g, e, 16 * g + e, 3] = plus
            z[i, g, (e + 8) % 16, 16 * g + e, 0] = minus
    return d
def setup_inputs(rng):
    return {**numbers_of(rng), **weights(rng, f(rng, N, 128, 2048))}
def setup_inputs_near(rng):
    size = np.where(rng.permutation(N) < N // 2, 2.0 ** -30, 1.0)
    s = rng.choice([1.0, 1.0, -1.0, 0.0], (N, 8, 4, C))
    a, i = (1 << LB) - 1, np.arange(N)
    s[..., a] = -1
    s[i, :, i % 4, a] = 1
    s[..., a + 126] = -1
    s[..., a + 127] = 1
    return {**marked(rng, s, size), **still(rng, 64)}
def setup_inputs_flat(rng):
    s = np.zeros((N, 8, 4, C))
    for r in range(N):
        for i in range(4):
            k = rng.permutation(8) % 6
            for g in range(8):
                a = s[r, g, i]
                if k[g] == 5: a[:] = rng.choice([1.0, -1.0, 0.0], C)
                elif k[g] != 2:
                    a[:] = 1.0 if k[g] in (0, 4) else -1.0
                    if k[g] > 2: a[int(rng.integers(C))] *= -1.0
    d = marked(rng, s, np.ones(N))
    d["x"][int(rng.integers(N))] = 0
    return {**d, **still(rng, 64)}
def setup_inputs_huge(rng):
    d = numbers_of(rng)
    h = (np.arange(N) + int(rng.integers(4))) % 4
    c = rng.choice([-1.0, 1.0], (N, 8, C))
    c[:, :, 0] = 1
    c[:, :, 1] = -1
    c[h == 0] = c[h == 0][:, :1]
    c[h > 1] = 1
    x = 2.0 ** 30 * (0.65 + 0.1 * rng.random((N, 8, 16, C, 4))) * c[:, :, None, :, None]
    k = rng.choice([-1.0, 1.0], (N, 128, K, 4))
    k[:, :, ::2] = rng.choice([-1.0, 1.0], (N, 1, K // 2, 1))
    q = 2.0 ** 29 * (0.75 + 0.25 * rng.random((N, 128, K, 4))) * k
    s = rng.choice([-1.0, 1.0], (N, 8))
    s[h == 0] = -np.roll(s, -1, axis=0)[h == 0]
    s = np.maximum(np.eye(8), (h == 0)[:, None, None]) * s[:, None, :]
    u = d["u"].reshape(N, 8, 16, 128, 4)
    u[:, :, :, ::16] = (2.0 ** 30 * (0.9 + 0.1 * rng.random((N, 8, 16, 8, 4))) * s[:, :, None, :, None] + 0.0).astype(np.float32).astype(BF)
    z = 2.0 ** 30 * (0.75 + 0.25 * rng.random((N, 128, 128, 4))) * rng.choice([-1.0, 1.0], (N, 1, 128, 1))
    d["x"] = x.astype(np.float32).astype(BF).reshape(N, 128, 4 * C)
    d["q"] = q.astype(np.float32).astype(BF).reshape(N, 128, 4 * K)
    d["z"] = z.astype(np.float32).astype(BF).reshape(N, 128, 512)
    return {**d, **still(rng, 1)}
def setup_inputs_spread(rng):
    d = setup_inputs(rng)
    d["x"] = wide(rng, N, 128, 4 * C, cols=6)
    d["q"] = wide(rng, N, 128, 4 * K, cols=6)
    return d
def check_inputs(d):
    b = []
    for k in ("x", "q", "u", "z", "v"):
        a = np.abs(d[k].astype(np.float32))
        if not (np.isfinite(a).all() and ((a == 0) | (a >= 2.0 ** -30) & (a <= 2.0 ** 30)).all()): b.append("a value of " + k)
    return b
def reference(x, q, u, z, v, wc, ws):
    qu = [mx_ref.quantize(u[r]) for r in range(N)]
    lay = [pk(wc[r], ws[r]) for r in range(N)]
    y, ol = np.zeros((N, 128, K), np.float32), np.zeros((N, 8, K), np.float32)
    oc, osc = np.zeros((N, 128, 4 * K), np.uint8), np.zeros((N, 16, K), np.uint8)
    weight = (1 << np.arange(7))[:, None]
    for r in range(N):
        t, at, key = x[r], np.tile(np.arange(C), (8, 1)), np.zeros((8, C), np.int64)
        level, path = [], []
        for l in range(3):
            h = (r + l) % N
            if l:
                g = mx_ref.quantize(gcols(t, o))
                t = layer(lay[h], g, decode(g))
                at = np.take_along_axis(np.argsort(o, axis=1), at, axis=1)
            bit = mx_ref.matmul(qu[h], mx_ref.quantize(t))[::16] > 0
            o = np.argsort(bit, axis=1, kind="stable")
            key = 2 * key + np.take_along_axis(bit, at, axis=1)
            level.append(t)
            path.append(at)
        e = mx_ref.matmul(mx_ref.quantize(z[r]), mx_ref.quantize(q[r])).reshape(8, 16, K) > 0
        lo = np.sum(e[:, :LB] * weight[:LB], axis=1)
        k = np.sum(e[:, LB:LB + 7] * weight, axis=1)
        i = np.argsort(key[np.arange(8)[:, None, None], lo[:, :, None] + np.arange(128)], axis=2, kind="stable")
        a = lo + np.take_along_axis(i, k[:, :, None], axis=2)[:, :, 0]
        part = [gcols(level[l], np.take_along_axis(path[l], a, axis=1)) for l in range(3)]
        first = ((decode(mx_ref.quantize(part[2])) + decode(mx_ref.quantize(part[1]))) * np.float32(0.5)).astype(BF)
        both = ((decode(mx_ref.quantize(first)) + part[0].astype(np.float32)) * np.float32(0.5)).astype(BF)
        last = mx_ref.quantize(layer(lay[r], mx_ref.quantize(both), q[r].astype(np.float32)))
        y[r] = mx_ref.matmul(mx_ref.quantize(v[r]), last)
        ol[r] = a
        oc[r], osc[r] = emit(last)
    return {"y": y, "ol": ol, "oc": oc, "osc": osc}

@@ -1,0 +1,392 @@
+from concourse.mybir import dt, AluOpType, AxisListType, ActivationFunctionType
+
+C, K = 224, 48
+BF, F32, I32, U16, U8, MX = "bfloat16", "float32", "int32", "uint16", "uint8", "float8_e4m3fn_x4"
+SCRATCH = {}
+for _n, _w in dict(xt=4 * C, ut=512, zt=512, vt=512, qt=512, et=2048, zer=512, f0t=4 * C, t1t=4 * C, f1t=4 * C, t2t=4 * C,
+                   b1p=4 * C, b1t=512, xp=4 * C, bt=512, xxt=512, a0h=4 * K, q64=4 * K,
+                   t16=C, t4=C, ramp=C, u96=96, ident=128, m1=96, mb=C + 2, db=C + 2, dz=C + 2, mask4=C, keep4=C,
+                   ms=96, k16=96, k32=96, hm=96, k225=3 * (C + 1), twos=16,
+                   bit=C + 2, zi=C + 2, bm=C, yy=C, pp=C, oo=C, oex=C + 8, gx=96, gs=96,
+                   eb=96, etr=128, x1=3 * (C + 1), s1=3 * (C + 1), junk=3 * C,
+                   or1=C, or2=C, am=K, la=K).items():
+    SCRATCH[_n] = ("sbuf", [128, _w], BF)
+for _n, _w in dict(pf=8, pw=40, es=96, lh=6, wk=40, m0=12, m1s=12, lm0=12, lm1=12, th=20, tmp=4 * K, ys=K, arep=K).items():
+    SCRATCH[_n] = ("sbuf", [128, _w], F32)
+for _n, _w in dict(pc=16, vi=12).items():
+    SCRATCH[_n] = ("sbuf", [128, _w], I32)
+for _n, _w in dict(uoff=8, poff0=14, poff1=14, lp0=14, lp1=14, off4=56, woff=6, joff=4, aoff=4).items():
+    SCRATCH[_n] = ("sbuf", [128, _w], U16)
+for _n, _w in dict(lw=512, x0=C, u0=128, up=128, z0=128, q0=128, v0=128, e64=512, eh=512, f0=C, l0=C, t1=C, f1=C, l1=C, t2=C,
+                   b1=128, lb=128 + K, bb=128, xx=128).items():
+    SCRATCH[_n + "c"] = ("sbuf", [128, _w], MX)
+    SCRATCH[_n + "s"] = ("sbuf", [128, _w], U8)
+for _b in range(8):
+    SCRATCH["pb%d" % _b] = ("psum", [128, 512], F32)
+
+DMAS = ["x", "u", "q", "z", "wc", "ws", "v", "ol", "oc", "os0", "os1", "os2", "os3", "y"]
+ARRIVALS = ["p0", "f0", "m0", "p1", "f1", "m1", "a", "b1"]
+SEMAPHORES = ["cg", "cv", "ca", "cp", "sent"] + ["d_" + n for n in DMAS] + ["r_" + n for n in ARRIVALS]
+
+A = AluOpType
+ACT = ActivationFunctionType
+BIG = 255.0
+
+
+def rank_program(g, core, T, topo):
+    rank = T.rank_of(core)
+    if rank is None:
+        return
+    n = len(T.cores)
+    nxt, far = T.cores[(rank + 1) % n], T.cores[(rank + 2) % n]
+    prv = T.cores[(rank - 1) % n]
+    Q = {"g": g, "v": g.vector, "a": g.scalar, "p": g.tensor, "s": g.sync}
+    V, S, P = g.vector, g.scalar, g.tensor
+    ops, writer, readers = [], {}, {}
+    sent = [0]
+
+    def op(q, fn, r=(), w=(), sem=None):
+        deps = set()
+        w = list(w) + [k for k in r if k.startswith("pb")]
+        for k in r:
+            if k in writer:
+                deps.add(writer[k])
+        for k in w:
+            if k in writer:
+                deps.add(writer[k])
+            deps.update(readers.get(k, ()))
+        i = len(ops)
+        ops.append(dict(q=q, fn=fn, deps=deps, sem=sem))
+        for k in r:
+            readers.setdefault(k, []).append(i)
+        for k in w:
+            writer[k] = i
+            readers[k] = []
+
+    def arrival(name, src, calls, keys):
+        for k in keys:
+            writer[k] = len(ops)
+        ops.append(dict(q=None, deps=set(), sem="r_" + name, arr=calls * len(topo.engines(src, core))))
+
+    def dma(q, name, out, in_, r=(), w=()):
+        op(q, lambda: Q[q].dma_start(out, in_), r, w, sem="d_" + name)
+
+    def send(name, dst, out, in_, r):
+        rid, pid, _ = topo.addr(dst)
+        sent[0] += len(topo.engines(core, dst))
+        op("g", lambda: g.remote_dma(out, in_, T.sem["r_" + name], T.sem.sent, pid, rid, topo.mask(core, dst)), r, (), sem="sent")
+
+    def send_mx(name, dst, to, a, frm, cols):
+        send(name, dst, T[to + "c"][:, a:a + cols].bitcast(dt.uint8), T[frm + "c"][:, 0:cols].bitcast(dt.uint8), [frm])
+        send(name, dst, T[to + "s"][:, a:a + cols], T[frm + "s"][:, 0:cols], [frm])
+
+    def quant(name, tile, cols, r, key=None):
+        op("v", lambda: V.quantize_mx(T[name + "c"][:, 0:cols], T[name + "s"][:, 0:cols], tile), r, [key or name])
+
+    def mm(bank, st, a, mv, c0, cols, start, stop, r):
+        pb = "pb%d" % bank
+        op("p", lambda: P.matmul_mx(T[pb][:, 0:cols], T[st + "c"][:, a:a + 128], T[st + "s"][:, a:a + 128],
+                                    T[mv + "c"][:, c0:c0 + cols], T[mv + "s"][:, c0:c0 + cols], start, stop),
+           r, [pb] if start else [])
+        writer[pb] = len(ops) - 1
+
+    def ts(out, in0, s1, s2, o0, o1, r, w):
+        if o1 is None:
+            op("v", lambda: V.tensor_scalar(out, in0, s1, None, o0), r, w)
+        else:
+            op("v", lambda: V.tensor_scalar(out, in0, s1, s2, o0, o1), r, w)
+
+    def tt(out, in0, in1, o, r, w):
+        op("v", lambda: V.tensor_tensor(out, in0, in1, o), r, w)
+
+    def cp(out, in_, r, w):
+        op("v", lambda: V.tensor_copy(out, in_), r, w)
+
+    def scan(out, d0, d1, init, o0, o1, r, w):
+        op("v", lambda: V.tensor_tensor_scan(out, d0, d1, init, o0, o1), r, w)
+
+    def ms(ap, c, w):
+        op("v", lambda: V.memset(ap, c), (), w)
+
+    def act(out, in_, r, w, scale=None, bias=None):
+        if bias is not None:
+            op("a", lambda: S.activation(out, in_, ACT.Identity, bias=bias), r, w)
+        elif scale is not None:
+            op("a", lambda: S.activation(out, in_, ACT.Copy, scale=scale), r, w)
+        else:
+            op("a", lambda: S.activation(out, in_, ACT.Copy), r, w)
+
+    def iota(out, pattern, cm, w, small=True):
+        if small:
+            op("g", lambda: g.iota(out, pattern, 0, cm, allow_small_or_imprecise_dtypes=True), (), w)
+        else:
+            op("g", lambda: g.iota(out, pattern, 0, cm), (), w)
+
+    arrival("p0", far, 1, ["lp0"])
+    arrival("f0", prv, 2, ["l0"])
+    arrival("m0", prv, 1, ["lm0"])
+    arrival("p1", prv, 1, ["lp1"])
+    arrival("f1", prv, 2, ["l1"])
+    arrival("m1", prv, 1, ["lm1"])
+    arrival("a", far, 1, ["la"])
+    arrival("b1", far, 2, ["lb"])
+
+    dma("s", "u", T.ut[:], T.u[:], w=["ut"])
+    ms(T.mb[:, 0:C + 2:C + 1], BIG, ["mbe"])
+    ms(T.zer[:], 0.0, ["zer"])
+    dma("a", "x", T.xt[:], T.x[:], r=["mbe"], w=["xt"])
+    dma("s", "q", T.qt[:, 0:4 * K], T.q[:], r=["xt"], w=["qt"])
+    dma("s", "z", T.zt[:], T.z[:], w=["zt"])
+    dma("s", "wc", T.lwc[:].bitcast(dt.uint8), T.wc[:], w=["lw"])
+    dma("s", "ws", T.lws[:], T.ws[:], w=["lw2"])
+
+    iota(T.pc[:, 0:1], [[0, 1]], 1, ["pc0"], small=False)
+    iota(T.t16[:], [[0, C // 16], [1, 16]], 0, ["t16"])
+    iota(T.pc[:, 8:16], [[16, 8]], 0, ["u16i"], small=False)
+    iota(T.t4[:], [[0, C // 4], [1, 4]], 0, ["t4"])
+    iota(T.ramp[:], [[1, C]], 0, ["ramp"])
+    iota(T.u96[:], [[0, 3], [1, 2], [0, 16]], 0, ["u96"])
+    for b in range(4):
+        act(T.et[:, 512 * b:512 * (b + 1)], T.zer[:], ["zer"], ["et%d" % b])
+    ts(T.pc[:, 1:2], T.pc[:, 0:1], 15, None, A.bitwise_and, None, ["pc0"], ["pc1"])
+    ts(T.pc[:, 2:3], T.pc[:, 0:1], 3, None, A.bitwise_and, None, ["pc0"], ["pc2"])
+    ts(T.pc[:, 3:4], T.pc[:, 0:1], 2, 3, A.logical_shift_right, A.bitwise_and, ["pc0"], ["pc3"])
+    ts(T.pc[:, 4:5], T.pc[:, 0:1], 4, 1, A.logical_shift_right, A.bitwise_and, ["pc0"], ["pc4"])
+    ms(T.bit[:, C:C + 1], 1.0, ["bite"])
+    ms(T.keep4[:], 1.0, ["keep4"])
+    ms(T.twos[:], 2.0, ["twos"])
+    cp(T.pf[:, 0:5], T.pc[:, 0:5], ["pc0", "pc1", "pc2", "pc3", "pc4"], ["pf"])
+    ms(T.keep4[:, 0:C:4], 0.0, ["keep4"])
+    scan(T.pw[:, 0:16], T.twos[:], T.zer[:, 0:16], 0.5, A.mult, A.add, ["twos", "zer"], ["pw"])
+    ts(T.mb[:, 1:C + 1], T.t16[:], T.pf[:, 1:2], BIG, A.is_equal, A.mult, ["t16", "pf"], ["mb"])
+    ts(T.m1[:], T.t16[:, 0:96], T.pf[:, 1:2], None, A.is_equal, None, ["t16", "pf"], ["m1"])
+    cp(T.uoff[:], T.pc[:, 8:16], ["u16i"], ["uoff"])
+    tt(T.db[:, 0:C + 1], T.mb[:, 1:C + 2], T.mb[:, 0:C + 1], A.subtract, ["mb", "mbe"], ["db"])
+    tt(T.pw[:, 16:32], T.pw[:, 0:16], T.m1[:, 0:16], A.mult, ["pw", "m1"], ["pwm"])
+    ts(T.mask4[:], T.t4[:], T.pf[:, 3:4], None, A.is_equal, None, ["t4", "pf"], ["mask4"])
+    ts(T.dz[:, 0:C + 1], T.db[:, 0:C + 1], -1.0, 1.0, A.mult, A.add, ["db"], ["dz"])
+    op("v", lambda: V.tensor_reduce(T.pw[:, 32:33], T.pw[:, 16:29], AxisListType.X, A.add), ["pwm"], ["wcol"])
+
+    quant("u0", T.ut[:], 128, ["ut"])
+    op("v", lambda: V.tensor_copy(T.upc[:].bitcast(dt.uint32), T.u0c[:].bitcast(dt.uint32).indirect(T.uoff[:, 0:8])), ["u0", "uoff"], ["upa"])
+    op("a", lambda: S.activation(T.ups[:], T.u0s[:].indirect(T.uoff[:, 0:8]), ACT.Copy), ["u0", "uoff"], ["upb"])
+    ts(T.ident[:], T.ramp[:, 0:128], T.pf[:, 0:1], None, A.is_equal, None, ["ramp", "pf"], ["ident"])
+    quant("x0", T.xt[:], C, ["xt"])
+    ts(T.hm[:], T.u96[:], T.pf[:, 4:5], None, A.not_equal, None, ["u96", "pf"], ["hm"])
+
+    def order(tq, tile, tkeys, poff, pdst, ftile, fq, meanwhile):
+        mm(4, "up", 0, tq, 0, C, True, True, ["upa", "upb", tq])
+        ts(T.bit[:, 0:C], T.pb4[:, 0:C], 0.0, None, A.is_gt, None, ["pb4"], ["bit"])
+        meanwhile()
+        scan(T.zi[:, 0:C + 1], T.dz[:, 0:C + 1], T.bit[:, 0:C + 1], -1.0, A.add, A.subtract, ["dz", "bit", "bite"], ["zi"])
+        scan(T.bm[:], T.db[:, 0:C], T.bit[:, 0:C], T.zi[:, C:C + 1], A.add, A.add, ["db", "bit", "zi"], ["bm"])
+        scan(T.yy[:], T.bit[:, 0:C], T.zi[:, 0:C], BIG, A.mult, A.max, ["bit", "zi"], ["yy"])
+        scan(T.pp[:], T.bm[:], T.yy[:], 0.0, A.max, A.min, ["bm", "yy"], ["pp"])
+        cp(T[poff][:], T.pp[:, 15:C:16], ["pp"], [poff])
+        send(pdst[0], pdst[1], T["l" + pdst[0]][:], T[poff][:], [poff])
+        cp(T.oo[:].indirect(T[poff][:]), T.ramp[:], [poff, "ramp"], ["oo"])
+        scan(T.yy[:], T.oo[:], T.mask4[:], 0.0, A.max, A.mult, ["oo", "mask4"], ["yy"])
+        scan(T.pp[:], T.keep4[:], T.yy[:], 0.0, A.mult, A.add, ["keep4", "yy"], ["pp"])
+        ts(T.off4[:], T.pp[:, 3:C:4], 4.0, T.pf[:, 2:3], A.mult, A.add, ["pp", "pf"], ["off4"])
+        act(T[ftile][:, 2 * C:4 * C], T[tile][:].indirect(T.off4[:, 28:56]), ["off4"] + tkeys, [ftile + "b"])
+        cp(T[ftile][:, 0:2 * C], T[tile][:].indirect(T.off4[:, 0:28]), ["off4"] + tkeys, [ftile + "a"])
+        quant(fq, T[ftile][:], C, [ftile + "a", ftile + "b"])
+        send_mx(fq, nxt, "l" + fq[1], 0, fq, C)
+
+    def diagonals(c):
+        for b in range(4):
+            act(T.et[:, 513 * b:512 * (b + 1):4], T.ident[:], ["ident"], ["et%d" % b], scale=c)
+
+    def constants():
+        diagonals(64.0)
+        act(T.qt[:, 4 * K:512], T.zer[:, 4 * K:512], ["zer"], ["qtp"])
+        act(T.k225[:, 0:338], T.zer[:, 0:338], ["zer"], ["k225a"], bias=1.0)
+        act(T.k225[:, 338:675], T.zer[:, 0:337], ["zer"], ["k225b"], bias=1.0)
+        act(T.oex[:, 0:1], T.zer[:, 0:1], ["zer"], ["oexe"])
+        act(T.eb[:], T.zer[:, 0:96], ["zer"], ["eb"])
+        act(T.k225[:, 0:675:C + 1], T.zer[:, 0:3], ["zer", "k225a", "k225b"], ["k225"])
+
+    order("x0", "xt", ["xt"], "poff0", ("p0", far), "f0t", "f0", constants)
+    etk = ["et0", "et1", "et2", "et3"]
+    quant("q0", T.qt[:], 128, ["qt", "qtp"])
+    quant("z0", T.zt[:], 128, ["zt"])
+    quant("e64", T.et[:], 512, etk)
+
+    act(T.k32[:], T.zer[:, 0:96], ["zer"], ["k32a"], bias=1.0)
+    act(T.k16[:], T.zer[:, 0:96], ["zer"], ["k16a"], bias=1.0)
+    act(T.k32[:, 0:96:32], T.zer[:, 0:3], ["zer", "k32a"], ["k32"])
+    act(T.k16[:, 0:96:16], T.zer[:, 0:6], ["zer", "k16a"], ["k16"])
+    mm(6, "z0", 0, "q0", 0, 128, True, True, ["z0", "q0"])
+    ts(T.eb[:, 16:16 + K], T.pb6[:, 0:K], 0.0, T.pw[:, 32:33], A.is_gt, A.mult, ["pb6", "wcol"], ["eb"])
+    scan(T.oex[:, 1:C + 1], T.k225[:, 1:C + 1], T.bit[:, 0:C], 0.0, A.mult, A.add, ["k225", "bit"], ["oex"])
+    for k in range(4):
+        op("v", lambda k=k: V.transpose(T.etr[:, 32 * k:32 * k + 32], T.eb[:, 16 * k:16 * k + 32]), ["eb"], ["etr%d" % k])
+    tt(T.gx[:], T.etr[:, 16:112], T.hm[:], A.mult, ["etr0", "etr1", "etr2", "etr3", "hm"], ["gx"])
+    scan(T.es[:], T.k32[:], T.gx[:], 0.0, A.mult, A.add, ["k32", "gx"], ["es"])
+    cp(T.vi[:, 0:3], T.es[:, 31:96:32], ["es"], ["vi"])
+    ts(T.vi[:, 4:7], T.vi[:, 0:3], 63, None, A.bitwise_and, None, ["vi"], ["vlo"])
+    ts(T.vi[:, 8:11], T.vi[:, 0:3], 6, None, A.logical_shift_right, None, ["vi"], ["vk"])
+    cp(T.lh[:, 0:3], T.vi[:, 4:7], ["vlo"], ["lha"])
+    ts(T.lh[:, 3:6], T.vi[:, 4:7], 128.0, None, A.add, None, ["vlo"], ["lhb"])
+
+    def walk(lh, lhk, kk, kkey, out, okey):
+        W = T.wk
+        cp(T.woff[:], lh, lhk, ["woff"])
+        ts(W[:, 36:37], T.zi[:, C:C + 1], 1.0, None, A.add, None, ["zi"], ["wz"])
+        tt(T.gx[:], T.oex[:, 0:C + 1].indirect(T.woff[:]), T.m1[:], A.mult, ["oex", "oexe", "woff", "m1"], ["gx"])
+        scan(T.gs[:], T.k16[:], T.gx[:], 0.0, A.mult, A.add, ["k16", "gx"], ["gs"])
+        ab = T.gs[:, 15:96:16]
+        tt(W[:, 0:6], lh, ab, A.subtract, lhk + ["gs"], ["w0"])
+        ts(W[:, 6:12], ab, W[:, 36:37], None, A.add, None, ["gs", "wz"], ["w1"])
+        tt(W[:, 12:15], W[:, 3:6], W[:, 0:3], A.subtract, ["w0"], ["wn"])
+        tt(W[:, 24:30], W[:, 6:12], W[:, 0:6], A.subtract, ["w0", "w1"], ["wd"])
+        tt(W[:, 16:19], kk, W[:, 12:15], A.is_ge, [kkey, "wn"], ["wc0"])
+        tt(W[:, 19:22], kk, W[:, 12:15], A.is_ge, [kkey, "wn"], ["wc1"])
+        tt(W[:, 30:33], W[:, 16:19], W[:, 12:15], A.mult, ["wc0", "wn"], ["wcz"])
+        tt(W[:, 24:30], W[:, 24:30], W[:, 16:22], A.mult, ["wd", "wc0", "wc1"], ["wd"])
+        tt(out[:, 6:9], kk, W[:, 30:33], A.subtract, [kkey, "wcz"], [okey + "k"])
+        tt(out[:, 0:6], W[:, 0:6], W[:, 24:30], A.add, ["w0", "wd"], [okey + "l"])
+
+    walk(T.lh[:], ["lha", "lhb"], T.vi[:, 8:11], "vk", T.m0, "m0")
+    send("m0", nxt, T.lm0[:, 0:9], T.m0[:, 0:9], ["m0k", "m0l"])
+    dma("s", "v", T.vt[:], T.v[:], r=["l0"], w=["vt"])
+
+    def layer(land, tile, on_vector):
+        for b in range(4):
+            mm(b, "lw", 128 * b, land, 0, C, True, False, ["lw", "lw2", land])
+            mm(b, "e64", 128 * b, land, 0, C, False, True, ["e64", land])
+        for b in range(4):
+            out, src = T[tile][:, b:4 * C:4], T["pb%d" % b][:, 0:C]
+            if b in on_vector:
+                ts(out, src, 2.0 ** -6, None, A.mult, None, ["pb%d" % b], [tile + str(b)])
+            else:
+                act(out, src, ["pb%d" % b], [tile + str(b)], scale=2.0 ** -6)
+        return [tile + str(b) for b in range(4)]
+
+    keys = layer("l0", "t1t", ())
+    quant("t1", T.t1t[:], C, keys)
+    order("t1", "t1t", keys, "poff1", ("p1", nxt), "f1t", "f1", lambda: None)
+    scan(T.oex[:, 1:C + 1], T.k225[:, 1:C + 1], T.bit[:, 0:C], 0.0, A.mult, A.add, ["k225", "bit"], ["oex"])
+    walk(T.lm0[:, 0:6], ["lm0"], T.lm0[:, 6:9], "lm0", T.m1s, "m1")
+    tt(T.wk[:, 33:36], T.m1s[:, 0:3], T.m1s[:, 6:9], A.add, ["m1k", "m1l"], ["wlk"])
+    ts(T.m1s[:, 6:9], T.wk[:, 33:36], 0.5, None, A.add, None, ["wlk"], ["m1k"])
+    tt(T.m1s[:, 9:12], T.m1s[:, 6:9], T.m1s[:, 3:6], A.subtract, ["m1k", "m1l"], ["m1w"])
+    send("m1", nxt, T.lm1[:], T.m1s[:], ["m1k", "m1l", "m1w"])
+    cp(T.or1[:].indirect(T.lp0[:]), T.ramp[:], ["lp0", "ramp"], ["or1"])
+    cp(T.or2[:].indirect(T.lp1[:]), T.or1[:], ["lp1", "or1"], ["or2"])
+    act(T.ms[:, 0:K], T.m1[:, 0:K], ["m1"], ["msa"], scale=-1.0)
+    act(T.ms[:, K:96], T.m1[:, 0:K], ["m1"], ["msb"])
+    act(T.x1[:, 0:675:C + 1], T.zer[:, 0:3], ["zer"], ["x1e"], bias=-float(C))
+    act(T.b1t[:, 4 * K:512], T.zer[:, 4 * K:512], ["zer"], ["b1tp"])
+    for b in range(4):
+        act(T.xp[:, C * b:C * (b + 1)], T.xt[:, b:4 * C:4], ["xt"], ["xp%d" % b])
+
+    keys = layer("l1", "t2t", (2,))
+    banks = [5, 6, 7, 0]
+    for b in range(3):
+        mm(banks[b], "e64", 128 * b, "l1", 0, C, True, False, ["e64", "l1"])
+    quant("t2", T.t2t[:], C, keys)
+    cp(T.woff[:], T.lm1[:, 0:6], ["lm1"], ["woff"])
+    mm(4, "up", 0, "t2", 0, C, True, True, ["upa", "upb", "t2"])
+    for b in range(3):
+        mm(banks[b], "e64", 128 * b, "t2", 0, C, False, True, ["e64", "t2"])
+    mm(0, "e64", 384, "l1", 0, C, True, False, ["e64", "l1"])
+    mm(0, "e64", 384, "t2", 0, C, False, True, ["e64", "t2"])
+    for b in range(4):
+        act(T.b1p[:, C * b:C * (b + 1)], T["pb%d" % banks[b]][:, 0:C], ["pb%d" % banks[b]], ["b1p%d" % b], scale=2.0 ** -7)
+    ts(T.bit[:, 0:C], T.pb4[:, 0:C], 0.0, None, A.is_gt, None, ["pb4"], ["bit"])
+    scan(T.oex[:, 1:C + 1], T.k225[:, 1:C + 1], T.bit[:, 0:C], 0.0, A.mult, A.add, ["k225", "bit"], ["oex"])
+    scan(T.zi[:, 0:C], T.k225[:, 1:C + 1], T.bit[:, 0:C], 0.0, A.add, A.subtract, ["k225", "bit"], ["zi"])
+    tt(T.gx[:], T.oex[:, 0:C + 1].indirect(T.woff[:]), T.ms[:], A.mult, ["oex", "oexe", "woff", "msa", "msb"], ["gx"])
+    scan(T.gs[:], T.k16[:], T.gx[:], 0.0, A.mult, A.add, ["k16", "gx"], ["gs"])
+    tt(T.th[:, 0:6], T.gs[:, 15:96:16], T.lm1[:, 6:12], A.add, ["gs", "lm1"], ["th"])
+    for s in range(3):
+        op("a", lambda s=s: S.activation(T.junk[:, C * s:C * (s + 1)], T.zi[:, 0:C], ACT.Sign, bias=T.th[:, s:s + 1], scale=-1.0,
+                                         accum_out=T.th[:, 16 + s:17 + s]), ["zi", "th"], ["s0%d" % s])
+        ts(T.x1[:, (C + 1) * s + 1:(C + 1) * (s + 1)], T.oex[:, 1:C + 1], T.th[:, 3 + s:4 + s], 2.0, A.is_le, A.mult, ["oex", "th"], ["x1%d" % s])
+    tt(T.th[:, 6:9], T.th[:, 3:6], T.gs[:, 15:K:16], A.add, ["gs", "th"], ["dd"])
+    scan(T.s1[:], T.k225[:], T.x1[:], 0.0, A.mult, A.add, ["k225", "x1e", "x10", "x11", "x12"], ["s1"])
+    ts(T.th[:, 9:12], T.th[:, 6:9], -1000.0, None, A.mult, None, ["dd"], ["cap"])
+    tt(T.th[:, 12:15], T.th[:, 16:19], T.th[:, 9:12], A.min, ["cap", "s00", "s01", "s02"], ["low"])
+    tt(T.th[:, 6:9], T.s1[:, C:675:C + 1], T.th[:, 12:15], A.max, ["s1", "low"], ["dd"])
+    ts(T.joff[:, 0:3], T.th[:, 6:9], 0.5, C / 2.0, A.mult, A.add, ["dd"], ["joff"])
+    tt(T.am[:], T.or2[:].indirect(T.joff[:, 0:3]), T.ms[:, K:96], A.mult, ["or2", "joff", "msb"], ["am"])
+    send("a", far, T.la[:], T.am[:], ["am"])
+    for b in range(4):
+        src = T.b1p[:, C * b:C * (b + 1)].indirect(T.joff[:, 0:3])
+        (cp if b < 2 else act)(T.b1t[:, b:4 * K:4], src, ["b1p%d" % b, "joff"], ["b1t%d" % b])
+    quant("b1", T.b1t[:], 128, ["b1t0", "b1t1", "b1t2", "b1t3", "b1tp"])
+    send_mx("b1", far, "lb", 128, "b1", K)
+
+    diagonals(0.5)
+    act(T.bt[:, 4 * K:512], T.zer[:, 4 * K:512], ["zer"], ["btp"])
+    act(T.xxt[:, 4 * K:512], T.zer[:, 4 * K:512], ["zer"], ["xxtp"])
+    act(T.q64[:], T.qt[:, 0:4 * K], ["qt"], ["q64"], scale=64.0)
+    quant("lb", T.zer[:], 128, ["zer"], key="lbz")
+    quant("v0", T.vt[:], 128, ["vt"])
+    quant("eh", T.et[:], 512, etk)
+    scan(T.gs[:, 0:K], T.k16[:, 0:K], T.la[:], 0.0, A.mult, A.add, ["k16", "la"], ["gs"])
+    cp(T.aoff[:, 0:3], T.gs[:, 15:K:16], ["gs"], ["aoff"])
+    for b in range(4):
+        src, out = T.xp[:, C * b:C * (b + 1)].indirect(T.aoff[:, 0:3]), T.a0h[:, K * b:K * (b + 1)]
+        if b < 2:
+            ts(out, src, 0.5, None, A.mult, None, ["xp%d" % b, "aoff"], ["a0h%d" % b])
+        else:
+            act(out, src, ["xp%d" % b, "aoff"], ["a0h%d" % b], scale=0.5)
+    act(T.arep[:], T.ramp[:].indirect(T.aoff[:, 0:3]), ["ramp", "aoff"], ["arep"])
+    dma("s", "ol", T.ol[:], T.arep[0:128:16, :], r=["arep"])
+    for b in range(4):
+        mm(b, "eh", 128 * b, "lb", K, 128, True, True, ["eh", "lb", "lbz"])
+    for b in range(4):
+        tt(T.bt[:, b:4 * K:4], T["pb%d" % b][:, 128 - K:128], T.a0h[:, K * b:K * (b + 1)], A.add, ["pb%d" % b, "a0h%d" % b], ["bt%d" % b])
+    quant("bb", T.bt[:], 128, ["bt0", "bt1", "bt2", "bt3", "btp"])
+    for b in range(4):
+        mm(4 + b, "lw", 128 * b, "bb", 0, 128, True, True, ["lw", "lw2", "bb"])
+    for b in range(4):
+        tt(T.tmp[:, b:4 * K:4], T["pb%d" % (4 + b)][:, 0:K], T.q64[:, b:4 * K:4], A.add, ["pb%d" % (4 + b), "q64"], ["tmp%d" % b])
+    ts(T.xxt[:, 0:4 * K], T.tmp[:], 2.0 ** -6, None, A.mult, None, ["tmp0", "tmp1", "tmp2", "tmp3"], ["xxt"])
+    quant("xx", T.xxt[:], 128, ["xxt", "xxtp"])
+    mm(0, "v0", 0, "xx", 0, 128, True, True, ["v0", "xx"])
+    dma("s", "oc", T.oc[:], T.xxc[:, 0:K].bitcast(dt.uint8), r=["xx"])
+    for k in range(4):
+        dma("s" if k < 2 else "a", "os%d" % k, T.osc[4 * k:4 * k + 4, :], T.xxs[32 * k:32 * k + 4, 0:K], r=["xx"])
+    cp(T.ys[:], T.pb0[:, 0:K], ["pb0"], ["ys"])
+    dma("a", "y", T.y[:], T.ys[:], r=["ys"])
+
+    needed = set()
+    for o in ops:
+        needed.update(o["deps"])
+    count, token, known = {}, {}, {q: {} for q in Q}
+    for i, o in enumerate(ops):
+        if o["q"] is None:
+            token[i] = (o["sem"], o["arr"], {})
+            continue
+        q, kn = o["q"], known[o["q"]]
+        want = {}
+        for d in o["deps"]:
+            s, v, _ = token[d]
+            want[s] = max(want.get(s, 0), v)
+        for d in sorted(o["deps"], reverse=True):
+            s, v, clock = token[d]
+            if want[s] == v and kn.get(s, 0) < v:
+                Q[q].wait_ge(T.sem[s], v)
+                kn[s] = v
+            for s2, v2 in clock.items():
+                if kn.get(s2, 0) < v2:
+                    kn[s2] = v2
+        ins = o["fn"]()
+        if o["sem"] == "sent":
+            continue
+        if o["sem"]:
+            ins.then_inc(T.sem[o["sem"]], 16)
+            count[o["sem"]] = 16
+            token[i] = (o["sem"], 16, dict(kn))
+        elif i in needed:
+            s = "c" + q
+            ins.then_inc(T.sem[s], 1)
+            count[s] = count.get(s, 0) + 1
+            token[i] = (s, count[s], dict(kn))
+    count["sent"] = sent[0]
+    for s in sorted(count, key=lambda s: (s.startswith("d_o") or s == "d_y", s)):
+        if not any(known[q].get(s, 0) >= count[s] for q in Q):
+            g.wait_ge(T.sem[s], count[s])

@@ -1,23 +1,23 @@
-from concourse.mybir import dt, AluOpType, AxisListType, ActivationFunctionType
+from concourse.mybir import dt, AluOpType, ActivationFunctionType
 
 C, K = 224, 48
+H = 128
 BF, F32, I32, U16, U8, MX = "bfloat16", "float32", "int32", "uint16", "uint8", "float8_e4m3fn_x4"
 SCRATCH = {}
-for _n, _w in dict(xt=4 * C, ut=512, zt=512, vt=512, qt=512, et=2048, zer=512, f0t=4 * C, t1t=4 * C, f1t=4 * C, t2t=4 * C,
+for _n, _w in dict(xt=4 * C, ut=512, zt=512, vt=512, qraw=4 * K, qt=512, et=516, zer=516, f0t=1024, t1t=1024, f1t=1024, t2t=1024,
                    b1p=4 * C, b1t=512, xp=4 * C, bt=512, xxt=512, a0h=4 * K, q64=4 * K,
-                   t16=C, t4=C, ramp=C, u96=96, ident=128, m1=96, mb=C + 2, db=C + 2, dz=C + 2, mask4=C, keep4=C,
-                   ms=96, k16=96, k32=96, hm=96, k225=3 * (C + 1), twos=16,
-                   bit=C + 2, zi=C + 2, bm=C, yy=C, pp=C, oo=C, oex=C + 8, gx=96, gs=96,
-                   eb=96, etr=128, x1=3 * (C + 1), s1=3 * (C + 1), junk=3 * C,
-                   or1=C, or2=C, am=K, la=K).items():
+                   t16=C, ramp=C + 2, mneg=96, mb=C + 2, db=C + 2, dz=C + 4, c4=C,
+                   ms=96, k16=K, kw=192, kq=192, k225=3 * (C + 1), twos=16,
+                   bit=C + 4, zi=C + 4, bm=C, yy=C, pp=C, oo=C, oex=C + 8, oex2=C + 8, gxa=192, gxb=192, gs=192,
+                   eb=192, etr=192, x1=3 * (C + 1), s1=3 * (C + 1), junk=3 * C,
+                   or1=C, or2=C, am=K, la=K, m0=10, m1s=12, lm0=10, lm1=12).items():
     SCRATCH[_n] = ("sbuf", [128, _w], BF)
-for _n, _w in dict(pf=8, pw=40, es=96, lh=6, wk=40, m0=12, m1s=12, lm0=12, lm1=12, th=20, tmp=4 * K, ys=K, arep=K).items():
+for _n, _w in dict(pf=24, pw=40, wk=40, th=20, tmp=4 * K, ys=K, arep=K).items():
     SCRATCH[_n] = ("sbuf", [128, _w], F32)
-for _n, _w in dict(pc=16, vi=12).items():
-    SCRATCH[_n] = ("sbuf", [128, _w], I32)
+SCRATCH["pc"] = ("sbuf", [128, 16], I32)
 for _n, _w in dict(uoff=8, poff0=14, poff1=14, lp0=14, lp1=14, off4=56, woff=6, joff=4, aoff=4).items():
     SCRATCH[_n] = ("sbuf", [128, _w], U16)
-for _n, _w in dict(lw=512, x0=C, u0=128, up=128, z0=128, q0=128, v0=128, e64=512, eh=512, f0=C, l0=C, t1=C, f1=C, l1=C, t2=C,
+for _n, _w in dict(lw=512, x0=C, u0=128, up=128, z0=128, q0=128, v0=128, e64=512, eh=512, f0=256, l0=C, t1=256, f1=256, l1=C, t2=256,
                    b1=128, lb=128 + K, bb=128, xx=128).items():
     SCRATCH[_n + "c"] = ("sbuf", [128, _w], MX)
     SCRATCH[_n + "s"] = ("sbuf", [128, _w], U8)
@@ -25,12 +25,13 @@ for _b in range(8):
     SCRATCH["pb%d" % _b] = ("psum", [128, 512], F32)
 
 DMAS = ["x", "u", "q", "z", "wc", "ws", "v", "ol", "oc", "os0", "os1", "os2", "os3", "y"]
-ARRIVALS = ["p0", "f0", "m0", "p1", "f1", "m1", "a", "b1"]
+ARRIVALS = ["p0", "f0a", "f0b", "m0", "p1", "f1a", "f1b", "m1", "a", "b1"]
 SEMAPHORES = ["cg", "cv", "ca", "cp", "sent"] + ["d_" + n for n in DMAS] + ["r_" + n for n in ARRIVALS]
 
 A = AluOpType
 ACT = ActivationFunctionType
 BIG = 255.0
+MID = C / 2
 
 
 def rank_program(g, core, T, topo):
@@ -47,10 +48,11 @@ def rank_program(g, core, T, topo):
 
     def op(q, fn, r=(), w=(), sem=None):
         deps = set()
-        w = list(w) + [k for k in r if k.startswith("pb")]
         for k in r:
             if k in writer:
                 deps.add(writer[k])
+            if k.startswith("pb"):
+                deps.update(j for j in readers.get(k, ()) if ops[j]["q"] != q)
         for k in w:
             if k in writer:
                 deps.add(writer[k])
@@ -76,12 +78,14 @@ def rank_program(g, core, T, topo):
         sent[0] += len(topo.engines(core, dst))
         op("g", lambda: g.remote_dma(out, in_, T.sem["r_" + name], T.sem.sent, pid, rid, topo.mask(core, dst)), r, (), sem="sent")
 
-    def send_mx(name, dst, to, a, frm, cols):
-        send(name, dst, T[to + "c"][:, a:a + cols].bitcast(dt.uint8), T[frm + "c"][:, 0:cols].bitcast(dt.uint8), [frm])
-        send(name, dst, T[to + "s"][:, a:a + cols], T[frm + "s"][:, 0:cols], [frm])
+    def send_codes(name, dst, to, a, frm, b, cols, r):
+        send(name, dst, T[to + "c"][:, a:a + cols].bitcast(dt.uint8), T[frm + "c"][:, b:b + cols].bitcast(dt.uint8), r)
 
-    def quant(name, tile, cols, r, key=None):
-        op("v", lambda: V.quantize_mx(T[name + "c"][:, 0:cols], T[name + "s"][:, 0:cols], tile), r, [key or name])
+    def send_scales(name, dst, to, a, frm, b, cols, r):
+        send(name, dst, T[to + "s"][:, a:a + cols], T[frm + "s"][:, b:b + cols], r)
+
+    def quant(name, a, tile, cols, r, key=None):
+        op("v", lambda: V.quantize_mx(T[name + "c"][:, a:a + cols], T[name + "s"][:, a:a + cols], tile), r, [key or name])
 
     def mm(bank, st, a, mv, c0, cols, start, stop, r):
         pb = "pb%d" % bank
@@ -110,11 +114,14 @@ def rank_program(g, core, T, topo):
 
     def act(out, in_, r, w, scale=None, bias=None):
         if bias is not None:
-            op("a", lambda: S.activation(out, in_, ACT.Identity, bias=bias), r, w)
+            op("a", lambda: S.activation(out, in_, ACT.Identity, bias=bias, scale=1.0 if scale is None else scale), r, w)
         elif scale is not None:
             op("a", lambda: S.activation(out, in_, ACT.Copy, scale=scale), r, w)
         else:
             op("a", lambda: S.activation(out, in_, ACT.Copy), r, w)
+
+    def fill(out, cols, c, r, w):
+        act(out, T.zer[:, 0:cols], ["zer"] + r, w, bias=c)
 
     def iota(out, pattern, cm, w, small=True):
         if small:
@@ -123,209 +130,277 @@ def rank_program(g, core, T, topo):
             op("g", lambda: g.iota(out, pattern, 0, cm), (), w)
 
     arrival("p0", far, 1, ["lp0"])
-    arrival("f0", prv, 2, ["l0"])
+    arrival("f0a", prv, 2, ["l0a"])
+    arrival("f0b", prv, 1, ["l0b"])
     arrival("m0", prv, 1, ["lm0"])
     arrival("p1", prv, 1, ["lp1"])
-    arrival("f1", prv, 2, ["l1"])
+    arrival("f1a", prv, 2, ["l1a"])
+    arrival("f1b", prv, 1, ["l1b"])
     arrival("m1", prv, 1, ["lm1"])
     arrival("a", far, 1, ["la"])
     arrival("b1", far, 2, ["lb"])
 
     dma("s", "u", T.ut[:], T.u[:], w=["ut"])
-    ms(T.mb[:, 0:C + 2:C + 1], BIG, ["mbe"])
+    ms(T.mb[:, C:C + 1], BIG, ["mbe"])
     ms(T.zer[:], 0.0, ["zer"])
     dma("a", "x", T.xt[:], T.x[:], r=["mbe"], w=["xt"])
-    dma("s", "q", T.qt[:, 0:4 * K], T.q[:], r=["xt"], w=["qt"])
+    dma("s", "q", T.qraw[:], T.q[:], r=["xt"], w=["qraw"])
     dma("s", "z", T.zt[:], T.z[:], w=["zt"])
     dma("s", "wc", T.lwc[:].bitcast(dt.uint8), T.wc[:], w=["lw"])
     dma("s", "ws", T.lws[:], T.ws[:], w=["lw2"])
 
-    iota(T.pc[:, 0:1], [[0, 1]], 1, ["pc0"], small=False)
+    pc, pf = T.pc, T.pf
+    iota(pc[:, 0:2], [[12, 2]], 1, ["pc0"], small=False)
+    iota(T.ramp[:], [[1, C + 2]], 0, ["ramp"])
+    iota(pc[:, 8:16], [[16, 8]], 0, ["u16i"], small=False)
     iota(T.t16[:], [[0, C // 16], [1, 16]], 0, ["t16"])
-    iota(T.pc[:, 8:16], [[16, 8]], 0, ["u16i"], small=False)
-    iota(T.t4[:], [[0, C // 4], [1, 4]], 0, ["t4"])
-    iota(T.ramp[:], [[1, C]], 0, ["ramp"])
-    iota(T.u96[:], [[0, 3], [1, 2], [0, 16]], 0, ["u96"])
-    for b in range(4):
-        act(T.et[:, 512 * b:512 * (b + 1)], T.zer[:], ["zer"], ["et%d" % b])
-    ts(T.pc[:, 1:2], T.pc[:, 0:1], 15, None, A.bitwise_and, None, ["pc0"], ["pc1"])
-    ts(T.pc[:, 2:3], T.pc[:, 0:1], 3, None, A.bitwise_and, None, ["pc0"], ["pc2"])
-    ts(T.pc[:, 3:4], T.pc[:, 0:1], 2, 3, A.logical_shift_right, A.bitwise_and, ["pc0"], ["pc3"])
-    ts(T.pc[:, 4:5], T.pc[:, 0:1], 4, 1, A.logical_shift_right, A.bitwise_and, ["pc0"], ["pc4"])
-    ms(T.bit[:, C:C + 1], 1.0, ["bite"])
-    ms(T.keep4[:], 1.0, ["keep4"])
-    ms(T.twos[:], 2.0, ["twos"])
-    cp(T.pf[:, 0:5], T.pc[:, 0:5], ["pc0", "pc1", "pc2", "pc3", "pc4"], ["pf"])
-    ms(T.keep4[:, 0:C:4], 0.0, ["keep4"])
-    scan(T.pw[:, 0:16], T.twos[:], T.zer[:, 0:16], 0.5, A.mult, A.add, ["twos", "zer"], ["pw"])
-    ts(T.mb[:, 1:C + 1], T.t16[:], T.pf[:, 1:2], BIG, A.is_equal, A.mult, ["t16", "pf"], ["mb"])
-    ts(T.m1[:], T.t16[:, 0:96], T.pf[:, 1:2], None, A.is_equal, None, ["t16", "pf"], ["m1"])
-    cp(T.uoff[:], T.pc[:, 8:16], ["u16i"], ["uoff"])
-    tt(T.db[:, 0:C + 1], T.mb[:, 1:C + 2], T.mb[:, 0:C + 1], A.subtract, ["mb", "mbe"], ["db"])
-    tt(T.pw[:, 16:32], T.pw[:, 0:16], T.m1[:, 0:16], A.mult, ["pw", "m1"], ["pwm"])
-    ts(T.mask4[:], T.t4[:], T.pf[:, 3:4], None, A.is_equal, None, ["t4", "pf"], ["mask4"])
-    ts(T.dz[:, 0:C + 1], T.db[:, 0:C + 1], -1.0, 1.0, A.mult, A.add, ["db"], ["dz"])
-    op("v", lambda: V.tensor_reduce(T.pw[:, 32:33], T.pw[:, 16:29], AxisListType.X, A.add), ["pwm"], ["wcol"])
 
-    quant("u0", T.ut[:], 128, ["ut"])
+    def diagonal(c):
+        ts(T.et[:, 3:515:4], T.ramp[:, 0:128], pf[:, 0:1], c, A.is_equal, A.mult, ["ramp", "pf", "et0"], ["et"])
+
+    def unit(name, b):
+        quant(name, 128 * b, T.et[:, 3 - b:515 - b], 128, ["et", "et0"], key=name + str(b))
+
+    act(T.et[:], T.zer[:], ["zer"], ["et0"])
+    fill(T.bit[:, C:C + 1], 1, 1.0, [], ["bite"])
+    fill(T.bit[:, C + 1:C + 3], 2, 0.0, [], ["bitf"])
+    fill(T.dz[:, C + 1:C + 2], 1, -BIG, [], ["dze"])
+    fill(T.dz[:, C + 2:C + 3], 1, BIG + 1, [], ["dzf"])
+    ts(pc[:, 2:4], pc[:, 0:2], 2, 3, A.logical_shift_right, A.bitwise_and, ["pc0"], ["pc2"])
+    ts(pc[:, 4:5], pc[:, 0:1], 15, None, A.bitwise_and, None, ["pc0"], ["pc4"])
+    ts(pc[:, 5:6], pc[:, 0:1], 3, None, A.bitwise_and, None, ["pc0"], ["pc5"])
+    ts(pc[:, 6:7], pc[:, 0:1], 4, 1, A.logical_shift_right, A.bitwise_and, ["pc0"], ["pc6"])
+    ms(T.twos[:], 2.0, ["twos"])
+    cp(pf[:, 0:7], pc[:, 0:7], ["pc0", "pc2", "pc4", "pc5", "pc6"], ["pf"])
+    scan(T.pw[:, 0:16], T.twos[:], T.zer[:, 0:16], 0.5, A.mult, A.add, ["twos", "zer"], ["pw"])
+    ts(pf[:, 7:8], pf[:, 2:3], 0.0, 1024.0, A.is_equal, A.mult, ["pf"], ["s4a"])
+    ts(T.pw[:, 16:32], T.ramp[:, 0:16], pf[:, 4:5], -1.0, A.is_equal, A.mult, ["ramp", "pf"], ["own16"])
+    act(pf[:, 9:10], pf[:, 5:6], ["pf"], ["o4"], bias=-4.0)
+    act(pf[:, 10:11], pf[:, 6:7], ["pf"], ["c16"], scale=-2.0 ** 30, bias=2.0 ** 30)
+    act(pf[:, 11:12], pf[:, 6:7], ["pf"], ["sq"], scale=-1.0, bias=-2.0 ** -30)
+    ts(pf[:, 12:16], T.ramp[:, 0:4], pf[:, 2:3], 256.0, A.is_equal, A.mult, ["ramp", "pf"], ["c4a"])
+    ts(pf[:, 16:20], T.ramp[:, 0:4], pf[:, 3:4], 2.0 ** -16, A.not_equal, A.max, ["ramp", "pf"], ["c4b"])
+    diagonal(64.0)
+    cp(T.uoff[:], pc[:, 8:16], ["u16i"], ["uoff"])
+    tt(pf[:, 20:24], pf[:, 12:16], pf[:, 16:20], A.max, ["c4a", "c4b"], ["c4c"])
+    ts(pf[:, 8:9], pf[:, 7:8], 2.0 ** -6, None, A.max, None, ["s4a"], ["s4"])
+    tt(T.pw[:, 16:32], T.pw[:, 16:32], T.pw[:, 0:16], A.mult, ["pw", "own16"], ["pwm"])
+    for t in range(4):
+        fill(T.c4[:, t:C:4], C // 4, pf[:, 20 + t:21 + t], ["c4c"], ["c4%d" % t])
+    unit("e64", 0)
+    unit("e64", 1)
+    ts(T.mb[:, 0:C], T.t16[:], pf[:, 4:5], BIG, A.is_equal, A.mult, ["t16", "pf"], ["mb"])
+
+    quant("u0", 0, T.ut[:], 128, ["ut"])
+    scan(T.db[:, 0:C + 1], T.mb[:, 0:C + 1], T.mb[:, 0:C + 1], 0.0, A.subtract, A.min, ["mb", "mbe"], ["db"])
     op("v", lambda: V.tensor_copy(T.upc[:].bitcast(dt.uint32), T.u0c[:].bitcast(dt.uint32).indirect(T.uoff[:, 0:8])), ["u0", "uoff"], ["upa"])
     op("a", lambda: S.activation(T.ups[:], T.u0s[:].indirect(T.uoff[:, 0:8]), ACT.Copy), ["u0", "uoff"], ["upb"])
-    ts(T.ident[:], T.ramp[:, 0:128], T.pf[:, 0:1], None, A.is_equal, None, ["ramp", "pf"], ["ident"])
-    quant("x0", T.xt[:], C, ["xt"])
-    ts(T.hm[:], T.u96[:], T.pf[:, 4:5], None, A.not_equal, None, ["u96", "pf"], ["hm"])
+    quant("x0", 0, T.xt[:], C, ["xt"])
+    mm(0, "up", 0, "x0", 0, C, True, True, ["upa", "upb", "x0"])
+    ts(T.dz[:, 0:C + 1], T.db[:, 0:C + 1], -1.0, 1.0, A.mult, A.add, ["db"], ["dz"])
+    unit("e64", 2)
+    ts(T.bit[:, 0:C], T.pb0[:, 0:C], 0.0, None, A.is_gt, None, ["pb0"], ["bita", "bitb"])
 
-    def order(tq, tile, tkeys, poff, pdst, ftile, fq, meanwhile):
-        mm(4, "up", 0, tq, 0, C, True, True, ["upa", "upb", tq])
-        ts(T.bit[:, 0:C], T.pb4[:, 0:C], 0.0, None, A.is_gt, None, ["pb4"], ["bit"])
-        meanwhile()
-        scan(T.zi[:, 0:C + 1], T.dz[:, 0:C + 1], T.bit[:, 0:C + 1], -1.0, A.add, A.subtract, ["dz", "bit", "bite"], ["zi"])
-        scan(T.bm[:], T.db[:, 0:C], T.bit[:, 0:C], T.zi[:, C:C + 1], A.add, A.add, ["db", "bit", "zi"], ["bm"])
-        scan(T.yy[:], T.bit[:, 0:C], T.zi[:, 0:C], BIG, A.mult, A.max, ["bit", "zi"], ["yy"])
+    def order(tile, tkeys, poff, pdst, ftile, fq):
+        bits = ["bita", "bitb"]
+        scan(T.zi[:, 0:C + 3], T.dz[:, 0:C + 3], T.bit[:, 0:C + 3], BIG - 1, A.add, A.subtract, ["dz", "dze", "dzf", "bite", "bitf"] + bits, ["zi"])
+        scan(T.bm[:], T.db[:, 0:C], T.bit[:, 0:C], T.zi[:, C + 1:C + 2], A.add, A.add, ["db", "zi"] + bits, ["bm"])
+        scan(T.yy[:], T.bit[:, 0:C], T.zi[:, 0:C], BIG, A.mult, A.max, ["zi"] + bits, ["yy"])
         scan(T.pp[:], T.bm[:], T.yy[:], 0.0, A.max, A.min, ["bm", "yy"], ["pp"])
         cp(T[poff][:], T.pp[:, 15:C:16], ["pp"], [poff])
         send(pdst[0], pdst[1], T["l" + pdst[0]][:], T[poff][:], [poff])
-        cp(T.oo[:].indirect(T[poff][:]), T.ramp[:], [poff, "ramp"], ["oo"])
-        scan(T.yy[:], T.oo[:], T.mask4[:], 0.0, A.max, A.mult, ["oo", "mask4"], ["yy"])
-        scan(T.pp[:], T.keep4[:], T.yy[:], 0.0, A.mult, A.add, ["keep4", "yy"], ["pp"])
-        ts(T.off4[:], T.pp[:, 3:C:4], 4.0, T.pf[:, 2:3], A.mult, A.add, ["pp", "pf"], ["off4"])
-        act(T[ftile][:, 2 * C:4 * C], T[tile][:].indirect(T.off4[:, 28:56]), ["off4"] + tkeys, [ftile + "b"])
-        cp(T[ftile][:, 0:2 * C], T[tile][:].indirect(T.off4[:, 0:28]), ["off4"] + tkeys, [ftile + "a"])
-        quant(fq, T[ftile][:], C, [ftile + "a", ftile + "b"])
-        send_mx(fq, nxt, "l" + fq[1], 0, fq, C)
+        cp(T.oo[:].indirect(T[poff][:]), T.ramp[:, 1:C + 1], [poff, "ramp"], ["oo"])
+        scan(T.yy[:], T.oo[:], T.c4[:], 0.0, A.max, A.mult, ["oo", "c40", "c41", "c42", "c43"], ["yy"])
+        ts(T.off4[:], T.yy[:, 3:C:4], pf[:, 8:9], pf[:, 9:10], A.mult, A.add, ["yy", "s4", "o4"], ["off4"])
+        win = T[tile][:, 0:4 * C]
+        for eng, a, b, key in ((act, 16, 32, "a1"), (cp, 0, 16, "a0")):
+            eng(T[ftile][:, 16 * a:16 * b], win.indirect(T.off4[:, a:b]), ["off4"] + tkeys, [ftile + key])
+        act(T[ftile][:, 16 * 40:16 * 56], win.indirect(T.off4[:, 40:56]), ["off4"] + tkeys, [ftile + "b1"])
+        quant(fq, 0, T[ftile][:, 0:4 * H], H, [ftile + "a0", ftile + "a1"], key=fq + "a")
+        send_codes(fq + "a", nxt, "l" + fq[1], 0, fq, 0, H, [fq + "a"])
+        cp(T[ftile][:, 16 * 32:16 * 40], win.indirect(T.off4[:, 32:40]), ["off4"] + tkeys, [ftile + "b0"])
+        quant(fq, H, T[ftile][:, 4 * H:8 * H], H, [ftile + "b0", ftile + "b1", ftile + "p"], key=fq + "b")
+        send_scales(fq + "a", nxt, "l" + fq[1], 0, fq, 0, C, [fq + "a", fq + "b"])
+        send_codes(fq + "b", nxt, "l" + fq[1], H, fq, H, C - H, [fq + "b"])
 
-    def diagonals(c):
-        for b in range(4):
-            act(T.et[:, 513 * b:512 * (b + 1):4], T.ident[:], ["ident"], ["et%d" % b], scale=c)
+    for t in ("f0t", "t1t"):
+        fill(T[t][:, 4 * C:8 * H], 8 * H - 4 * C, 0.0, [], [t + "p"])
+    fill(T.qt[:, 8 * K:512], 512 - 8 * K, 0.0, [], ["qtp"])
+    fill(T.k225[:, 0:338], 338, 1.0, [], ["k225a"])
+    fill(T.k225[:, 338:675], 337, 1.0, [], ["k225b"])
+    fill(T.oex[:, 0:1], 1, 0.0, [], ["oexe"])
+    fill(T.k225[:, 0:675:C + 1], 3, 0.0, ["k225a", "k225b"], ["k225"])
+    fill(T.kw[:], 192, 1.0, [], ["kwa"])
+    fill(T.kq[:], 192, 1.0, [], ["kqa"])
+    fill(T.gxa[:], 192, 0.0, [], ["gxa0"])
+    act(T.mneg[:], T.mb[:, 0:96], ["mb"], ["mneg"], scale=-1.0 / BIG)
+    for a, b, k in ((16, 22, 32), (22, 29, 33)):
+        op("a", lambda a=a, b=b, k=k: S.activation(T.junk[:, a:b], T.pw[:, a:b], ACT.Copy, accum_out=T.pw[:, k:k + 1]), ["pwm"], ["w%d" % k])
+    for s in range(6):
+        act(T.qt[:, 64 * s:64 * (s + 1)], T.qraw[:, 64 * (s // 2):64 * (s // 2 + 1)], ["qraw"], ["qt%d" % s])
 
-    def constants():
-        diagonals(64.0)
-        act(T.qt[:, 4 * K:512], T.zer[:, 4 * K:512], ["zer"], ["qtp"])
-        act(T.k225[:, 0:338], T.zer[:, 0:338], ["zer"], ["k225a"], bias=1.0)
-        act(T.k225[:, 338:675], T.zer[:, 0:337], ["zer"], ["k225b"], bias=1.0)
-        act(T.oex[:, 0:1], T.zer[:, 0:1], ["zer"], ["oexe"])
-        act(T.eb[:], T.zer[:, 0:96], ["zer"], ["eb"])
-        act(T.k225[:, 0:675:C + 1], T.zer[:, 0:3], ["zer", "k225a", "k225b"], ["k225"])
+    order("xt", ["xt"], "poff0", ("p0", far), "f0t", "f0")
 
-    order("x0", "xt", ["xt"], "poff0", ("p0", far), "f0t", "f0", constants)
-    etk = ["et0", "et1", "et2", "et3"]
-    quant("q0", T.qt[:], 128, ["qt", "qtp"])
-    quant("z0", T.zt[:], 128, ["zt"])
-    quant("e64", T.et[:], 512, etk)
+    quant("q0", 0, T.qt[:], 128, ["qtp"] + ["qt%d" % s for s in range(6)])
+    quant("z0", 0, T.zt[:], 128, ["zt"])
+    mm(7, "z0", 0, "q0", 0, 128, True, True, ["z0", "q0"])
+    unit("e64", 3)
+    fill(T.kw[:, 0:192:32], 6, 0.0, ["kwa"], ["kw"])
+    fill(T.kq[:, 0:192:32], 6, 0.0, ["kqa"], ["kq0"])
+    fill(T.kq[:, 16:192:32], 6, pf[:, 10:11], ["kqa", "c16"], ["kq1"])
+    scan(T.oex[:, 1:C + 1], T.k225[:, 1:C + 1], T.bit[:, 0:C], 0.0, A.mult, A.add, ["k225", "bita", "bitb"], ["oex"])
+    for k in range(2):
+        ts(T.eb[:, 96 * k:96 * (k + 1)], T.pb7[:, 0:96], 0.0, T.pw[:, 32 + k:33 + k], A.is_gt, A.mult, ["pb7", "w%d" % (32 + k)], ["eb%d" % k])
+    op("v", lambda: V.transpose(T.etr[:], T.eb[:]), ["eb0", "eb1"], ["etr"])
+    scan(T.eb[:], T.kq[:], T.etr[:], 0.0, A.mult, A.add, ["kq0", "kq1", "etr"], ["eb0", "eb1"])
+    W = T.wk
+    for k in range(2):
+        ts(T.woff[:, 3 * k:3 * k + 3], T.eb[:, 31:96:32], pf[:, 11:12], 128.0 * k, A.mult, A.add, ["eb0", "sq"], ["woff%d" % k])
+    for k in range(2):
+        ts(T.gxa[:, 96 * k + 31:96 * (k + 1):32], T.eb[:, 31:96:32], pf[:, 11:12], 128.0 * k, A.mult, A.add, ["eb0", "sq", "gxa0"], ["gxs%d" % k])
+    ts(W[:, 33:36], T.eb[:, 127:192:32], pf[:, 11:12], 2.0 ** -6, A.mult, A.mult, ["eb0", "sq"], ["k0"])
 
-    act(T.k32[:], T.zer[:, 0:96], ["zer"], ["k32a"], bias=1.0)
-    act(T.k16[:], T.zer[:, 0:96], ["zer"], ["k16a"], bias=1.0)
-    act(T.k32[:, 0:96:32], T.zer[:, 0:3], ["zer", "k32a"], ["k32"])
-    act(T.k16[:, 0:96:16], T.zer[:, 0:6], ["zer", "k16a"], ["k16"])
-    mm(6, "z0", 0, "q0", 0, 128, True, True, ["z0", "q0"])
-    ts(T.eb[:, 16:16 + K], T.pb6[:, 0:K], 0.0, T.pw[:, 32:33], A.is_gt, A.mult, ["pb6", "wcol"], ["eb"])
-    scan(T.oex[:, 1:C + 1], T.k225[:, 1:C + 1], T.bit[:, 0:C], 0.0, A.mult, A.add, ["k225", "bit"], ["oex"])
-    for k in range(4):
-        op("v", lambda k=k: V.transpose(T.etr[:, 32 * k:32 * k + 32], T.eb[:, 16 * k:16 * k + 32]), ["eb"], ["etr%d" % k])
-    tt(T.gx[:], T.etr[:, 16:112], T.hm[:], A.mult, ["etr0", "etr1", "etr2", "etr3", "hm"], ["gx"])
-    scan(T.es[:], T.k32[:], T.gx[:], 0.0, A.mult, A.add, ["k32", "gx"], ["es"])
-    cp(T.vi[:, 0:3], T.es[:, 31:96:32], ["es"], ["vi"])
-    ts(T.vi[:, 4:7], T.vi[:, 0:3], 63, None, A.bitwise_and, None, ["vi"], ["vlo"])
-    ts(T.vi[:, 8:11], T.vi[:, 0:3], 6, None, A.logical_shift_right, None, ["vi"], ["vk"])
-    cp(T.lh[:, 0:3], T.vi[:, 4:7], ["vlo"], ["lha"])
-    ts(T.lh[:, 3:6], T.vi[:, 4:7], 128.0, None, A.add, None, ["vlo"], ["lhb"])
-
-    def walk(lh, lhk, kk, kkey, out, okey):
-        W = T.wk
-        cp(T.woff[:], lh, lhk, ["woff"])
-        ts(W[:, 36:37], T.zi[:, C:C + 1], 1.0, None, A.add, None, ["zi"], ["wz"])
-        tt(T.gx[:], T.oex[:, 0:C + 1].indirect(T.woff[:]), T.m1[:], A.mult, ["oex", "oexe", "woff", "m1"], ["gx"])
-        scan(T.gs[:], T.k16[:], T.gx[:], 0.0, A.mult, A.add, ["k16", "gx"], ["gs"])
-        ab = T.gs[:, 15:96:16]
-        tt(W[:, 0:6], lh, ab, A.subtract, lhk + ["gs"], ["w0"])
-        ts(W[:, 6:12], ab, W[:, 36:37], None, A.add, None, ["gs", "wz"], ["w1"])
-        tt(W[:, 12:15], W[:, 3:6], W[:, 0:3], A.subtract, ["w0"], ["wn"])
-        tt(W[:, 24:30], W[:, 6:12], W[:, 0:6], A.subtract, ["w0", "w1"], ["wd"])
+    def walk(kk, kkey, out, okey):
+        x0, gs = T.gs[:, 31:192:32], T.gs
+        yield tt(T.gxa[:, 0:192:2], T.oex[:, 0:C + 1].indirect(T.woff[:]), T.mneg[:], A.mult, ["oex", "oexe", "woff0", "woff1", "mneg", "gxa0"], ["gxa"])
+        yield scan(gs[:], T.kw[:], T.gxa[:], 0.0, A.mult, A.add, ["kw", "gxa", "gxs0", "gxs1"], ["gs"])
+        tt(W[:, 12:15], gs[:, 127:192:32], gs[:, 31:96:32], A.subtract, ["gs"], ["wn"])
+        yield ts(W[:, 6:12], gs[:, 30:192:32], -1.0, T.zi[:, C + 2:C + 3], A.mult, A.add, ["gs", "zi"], ["w1"])
         tt(W[:, 16:19], kk, W[:, 12:15], A.is_ge, [kkey, "wn"], ["wc0"])
         tt(W[:, 19:22], kk, W[:, 12:15], A.is_ge, [kkey, "wn"], ["wc1"])
+        yield tt(W[:, 24:30], W[:, 6:12], x0, A.subtract, ["gs", "w1"], ["wd"])
         tt(W[:, 30:33], W[:, 16:19], W[:, 12:15], A.mult, ["wc0", "wn"], ["wcz"])
-        tt(W[:, 24:30], W[:, 24:30], W[:, 16:22], A.mult, ["wd", "wc0", "wc1"], ["wd"])
+        yield tt(W[:, 0:6], W[:, 24:30], W[:, 16:22], A.mult, ["wd", "wc0", "wc1"], ["we"])
         tt(out[:, 6:9], kk, W[:, 30:33], A.subtract, [kkey, "wcz"], [okey + "k"])
-        tt(out[:, 0:6], W[:, 0:6], W[:, 24:30], A.add, ["w0", "wd"], [okey + "l"])
+        yield tt(out[:, 0:6], W[:, 0:6], x0, A.add, ["gs", "we"], [okey + "l"])
 
-    walk(T.lh[:], ["lha", "lhb"], T.vi[:, 8:11], "vk", T.m0, "m0")
+    def steps(it, k):
+        for _ in range(k):
+            next(it, None)
+
+    def products(land, half):
+        c0, r = ((0, [land + "a"]), (C - H, [land + "a", land + "b"]))[half]
+        for b in range(4):
+            mm(4 * half + b, "lw", 128 * b, land, c0, H, True, False, ["lw", "lw2"] + r)
+            mm(4 * half + b, "e64", 128 * b, land, c0, H, False, True, ["e64%d" % b] + r)
+
+    def casts(tile, half):
+        a, b0, c0 = ((0, 4 * H, 0), (4 * H, 4 * C, 2 * H - C))[half]
+        for b in range(4):
+            pb = "pb%d" % (4 * half + b)
+            act(T[tile][:, a + b:b0:4], T[pb][:, c0:H], [pb], [tile + str(4 * half + b)], scale=2.0 ** -6)
+        return [tile + str(4 * half + b) for b in range(4)]
+
+    def scores(tq, half):
+        mm(half, "up", 0, tq, H * half, H, True, True, ["upa", "upb", tq + "ab"[half]])
+
+    def bits(half):
+        a, b = ((0, H), (H, C))[half]
+        ts(T.bit[:, a:b], T["pb%d" % half][:, 0:b - a], 0.0, None, A.is_gt, None, ["pb%d" % half], ["bit" + "ab"[half]])
+
+    w0 = walk(W[:, 33:36], "k0", T.m0, "m0")
+    steps(w0, 2)
+    cp(T.or1[:].indirect(T.lp0[:]), T.ramp[:, 0:C], ["lp0", "ramp"], ["or1"])
+    dma("s", "v", T.vt[:], T.v[:], r=["l0b"], w=["vt"])
+
+    products("l0", 0)
+    ka = casts("t1t", 0)
+    products("l0", 1)
+    kb = casts("t1t", 1)
+    quant("t1", 0, T.t1t[:, 0:4 * H], H, ka, key="t1a")
+    scores("t1", 0)
+    steps(w0, 2)
+    quant("t1", H, T.t1t[:, 4 * H:8 * H], H, kb + ["t1tp"], key="t1b")
+    scores("t1", 1)
+    steps(w0, 1)
+    bits(0)
+    steps(w0, 1)
     send("m0", nxt, T.lm0[:, 0:9], T.m0[:, 0:9], ["m0k", "m0l"])
-    dma("s", "v", T.vt[:], T.v[:], r=["l0"], w=["vt"])
-
-    def layer(land, tile, on_vector):
-        for b in range(4):
-            mm(b, "lw", 128 * b, land, 0, C, True, False, ["lw", "lw2", land])
-            mm(b, "e64", 128 * b, land, 0, C, False, True, ["e64", land])
-        for b in range(4):
-            out, src = T[tile][:, b:4 * C:4], T["pb%d" % b][:, 0:C]
-            if b in on_vector:
-                ts(out, src, 2.0 ** -6, None, A.mult, None, ["pb%d" % b], [tile + str(b)])
-            else:
-                act(out, src, ["pb%d" % b], [tile + str(b)], scale=2.0 ** -6)
-        return [tile + str(b) for b in range(4)]
-
-    keys = layer("l0", "t1t", ())
-    quant("t1", T.t1t[:], C, keys)
-    order("t1", "t1t", keys, "poff1", ("p1", nxt), "f1t", "f1", lambda: None)
-    scan(T.oex[:, 1:C + 1], T.k225[:, 1:C + 1], T.bit[:, 0:C], 0.0, A.mult, A.add, ["k225", "bit"], ["oex"])
-    walk(T.lm0[:, 0:6], ["lm0"], T.lm0[:, 6:9], "lm0", T.m1s, "m1")
-    tt(T.wk[:, 33:36], T.m1s[:, 0:3], T.m1s[:, 6:9], A.add, ["m1k", "m1l"], ["wlk"])
-    ts(T.m1s[:, 6:9], T.wk[:, 33:36], 0.5, None, A.add, None, ["wlk"], ["m1k"])
-    tt(T.m1s[:, 9:12], T.m1s[:, 6:9], T.m1s[:, 3:6], A.subtract, ["m1k", "m1l"], ["m1w"])
+    bits(1)
+    for t in ("f1t", "t2t"):
+        fill(T[t][:, 4 * C:8 * H], 8 * H - 4 * C, 0.0, [], [t + "p"])
+    fill(T.gxb[:], 192, 0.0, [], ["gxb0"])
+    fill(T.gxb[:, 1:96:32], 3, -MID, ["gxb0"], ["gxb1"])
+    fill(T.gxb[:, 97:192:32], 3, 0.5, ["gxb0"], ["gxb2"])
+    fill(T.oex2[:, 0:1], 1, -MID, [], ["oex2e"])
+    act(T.ms[:, 0:K], T.mneg[:, 0:K], ["mneg"], ["msa"])
+    act(T.ms[:, K:96], T.mneg[:, 0:K], ["mneg"], ["msb"], scale=-1.0)
+    order("t1t", ka + kb, "poff1", ("p1", nxt), "f1t", "f1")
+    scan(T.oex[:, 1:C + 1], T.k225[:, 1:C + 1], T.bit[:, 0:C], 0.0, A.mult, A.add, ["k225", "bita", "bitb"], ["oex"])
+    cp(T.woff[:], T.lm0[:, 0:6], ["lm0"], ["woff0", "woff1"])
+    cp(T.gxa[:, 31:192:32], T.lm0[:, 0:6], ["lm0"], ["gxs0", "gxs1"])
+    w1 = walk(T.lm0[:, 6:9], "lm0", T.m1s, "m1")
+    steps(w1, 6)
+    tt(W[:, 33:36], T.m1s[:, 0:3], T.m1s[:, 6:9], A.add, ["m1k", "m1l"], ["wlk"])
+    ts(T.m1s[:, 6:9], W[:, 33:36], 0.5 - MID, None, A.add, None, ["wlk"], ["m1k"])
+    tt(T.m1s[:, 9:12], W[:, 33:36], T.m1s[:, 3:6], A.subtract, ["wlk", "m1l"], ["m1w"])
     send("m1", nxt, T.lm1[:], T.m1s[:], ["m1k", "m1l", "m1w"])
-    cp(T.or1[:].indirect(T.lp0[:]), T.ramp[:], ["lp0", "ramp"], ["or1"])
-    cp(T.or2[:].indirect(T.lp1[:]), T.or1[:], ["lp1", "or1"], ["or2"])
-    act(T.ms[:, 0:K], T.m1[:, 0:K], ["m1"], ["msa"], scale=-1.0)
-    act(T.ms[:, K:96], T.m1[:, 0:K], ["m1"], ["msb"])
-    act(T.x1[:, 0:675:C + 1], T.zer[:, 0:3], ["zer"], ["x1e"], bias=-float(C))
-    act(T.b1t[:, 4 * K:512], T.zer[:, 4 * K:512], ["zer"], ["b1tp"])
+    fill(T.x1[:, 0:675:C + 1], 3, -float(C), [], ["x1e"])
+    fill(T.b1t[:, 4 * K:512], 512 - 4 * K, 0.0, [], ["b1tp"])
+    fill(T.k16[:], K, 1.0, [], ["k16a"])
+    fill(T.k16[:, 0:K:16], 3, 0.0, ["k16a"], ["k16"])
     for b in range(4):
         act(T.xp[:, C * b:C * (b + 1)], T.xt[:, b:4 * C:4], ["xt"], ["xp%d" % b])
 
-    keys = layer("l1", "t2t", (2,))
-    banks = [5, 6, 7, 0]
+    products("l1", 0)
+    ka = casts("t2t", 0)
+    products("l1", 1)
+    kb = casts("t2t", 1)
+    cp(T.or2[:].indirect(T.lp1[:]), T.or1[:], ["lp1", "or1"], ["or2"])
+    quant("t2", 0, T.t2t[:, 0:4 * H], H, ka, key="t2a")
+    scores("t2", 0)
+    banks = [2, 3, 4, 5]
     for b in range(3):
-        mm(banks[b], "e64", 128 * b, "l1", 0, C, True, False, ["e64", "l1"])
-    quant("t2", T.t2t[:], C, keys)
-    cp(T.woff[:], T.lm1[:, 0:6], ["lm1"], ["woff"])
-    mm(4, "up", 0, "t2", 0, C, True, True, ["upa", "upb", "t2"])
+        mm(banks[b], "e64", 128 * b, "l1", 0, C, True, False, ["e64%d" % b, "l1a", "l1b"])
+    quant("t2", H, T.t2t[:, 4 * H:8 * H], H, kb + ["t2tp"], key="t2b")
+    scores("t2", 1)
     for b in range(3):
-        mm(banks[b], "e64", 128 * b, "t2", 0, C, False, True, ["e64", "t2"])
-    mm(0, "e64", 384, "l1", 0, C, True, False, ["e64", "l1"])
-    mm(0, "e64", 384, "t2", 0, C, False, True, ["e64", "t2"])
-    for b in range(4):
+        mm(banks[b], "e64", 128 * b, "t2", 0, C, False, True, ["e64%d" % b, "t2a", "t2b"])
+    mm(banks[3], "e64", 384, "l1", 0, C, True, False, ["e643", "l1a", "l1b"])
+    mm(banks[3], "e64", 384, "t2", 0, C, False, True, ["e643", "t2a", "t2b"])
+
+    def halves(b):
         act(T.b1p[:, C * b:C * (b + 1)], T["pb%d" % banks[b]][:, 0:C], ["pb%d" % banks[b]], ["b1p%d" % b], scale=2.0 ** -7)
-    ts(T.bit[:, 0:C], T.pb4[:, 0:C], 0.0, None, A.is_gt, None, ["pb4"], ["bit"])
-    scan(T.oex[:, 1:C + 1], T.k225[:, 1:C + 1], T.bit[:, 0:C], 0.0, A.mult, A.add, ["k225", "bit"], ["oex"])
-    scan(T.zi[:, 0:C], T.k225[:, 1:C + 1], T.bit[:, 0:C], 0.0, A.add, A.subtract, ["k225", "bit"], ["zi"])
-    tt(T.gx[:], T.oex[:, 0:C + 1].indirect(T.woff[:]), T.ms[:], A.mult, ["oex", "oexe", "woff", "msa", "msb"], ["gx"])
-    scan(T.gs[:], T.k16[:], T.gx[:], 0.0, A.mult, A.add, ["k16", "gx"], ["gs"])
-    tt(T.th[:, 0:6], T.gs[:, 15:96:16], T.lm1[:, 6:12], A.add, ["gs", "lm1"], ["th"])
+
+    for b in range(3):
+        halves(b)
+    bits(0)
+    cp(T.woff[:], T.lm1[:, 0:6], ["lm1"], ["woff0", "woff1"])
+    cp(T.gxb[:, 31:192:32], T.lm1[:, 6:12], ["lm1", "gxb0"], ["gxbs"])
+    bits(1)
+    scan(T.oex2[:, 1:C + 1], T.k225[:, 1:C + 1], T.bit[:, 0:C], -MID, A.mult, A.add, ["k225", "bita", "bitb"], ["oex2"])
+    scan(T.zi[:, 0:C], T.k225[:, 1:C + 1], T.bit[:, 0:C], -MID, A.add, A.subtract, ["k225", "bita", "bitb"], ["zi"])
+    tt(T.gxb[:, 0:192:2], T.oex2[:, 0:C + 1].indirect(T.woff[:]), T.ms[:], A.mult, ["oex2", "oex2e", "woff0", "woff1", "msa", "msb", "gxb0"], ["gxb"])
+    scan(T.gs[:], T.kw[:], T.gxb[:], 0.0, A.mult, A.add, ["kw", "gxb", "gxb1", "gxb2", "gxbs"], ["gs"])
     for s in range(3):
-        op("a", lambda s=s: S.activation(T.junk[:, C * s:C * (s + 1)], T.zi[:, 0:C], ACT.Sign, bias=T.th[:, s:s + 1], scale=-1.0,
-                                         accum_out=T.th[:, 16 + s:17 + s]), ["zi", "th"], ["s0%d" % s])
-        ts(T.x1[:, (C + 1) * s + 1:(C + 1) * (s + 1)], T.oex[:, 1:C + 1], T.th[:, 3 + s:4 + s], 2.0, A.is_le, A.mult, ["oex", "th"], ["x1%d" % s])
-    tt(T.th[:, 6:9], T.th[:, 3:6], T.gs[:, 15:K:16], A.add, ["gs", "th"], ["dd"])
+        op("a", lambda s=s: S.activation(T.junk[:, C * s:C * (s + 1)], T.zi[:, 0:C], ACT.Sign, bias=T.gs[:, 32 * s + 31:32 * s + 32], scale=-1.0,
+                                         accum_out=T.th[:, 16 + s:17 + s]), ["zi", "gs"], ["s0%d" % s])
+        ts(T.x1[:, (C + 1) * s + 1:(C + 1) * (s + 1)], T.oex2[:, 1:C + 1], T.gs[:, 32 * s + 127:32 * s + 128], 2.0, A.is_le, A.mult, ["oex2", "gs"], ["x1%d" % s])
+    halves(3)
+    tt(T.th[:, 6:9], T.gs[:, 127:192:32], T.gs[:, 30:96:32], A.add, ["gs"], ["dd"])
     scan(T.s1[:], T.k225[:], T.x1[:], 0.0, A.mult, A.add, ["k225", "x1e", "x10", "x11", "x12"], ["s1"])
-    ts(T.th[:, 9:12], T.th[:, 6:9], -1000.0, None, A.mult, None, ["dd"], ["cap"])
+    ts(T.th[:, 9:12], T.th[:, 6:9], MID, -1000.0, A.add, A.mult, ["dd"], ["cap"])
     tt(T.th[:, 12:15], T.th[:, 16:19], T.th[:, 9:12], A.min, ["cap", "s00", "s01", "s02"], ["low"])
     tt(T.th[:, 6:9], T.s1[:, C:675:C + 1], T.th[:, 12:15], A.max, ["s1", "low"], ["dd"])
-    ts(T.joff[:, 0:3], T.th[:, 6:9], 0.5, C / 2.0, A.mult, A.add, ["dd"], ["joff"])
+    ts(T.joff[:, 0:3], T.th[:, 6:9], 0.5, MID, A.mult, A.add, ["dd"], ["joff"])
     tt(T.am[:], T.or2[:].indirect(T.joff[:, 0:3]), T.ms[:, K:96], A.mult, ["or2", "joff", "msb"], ["am"])
     send("a", far, T.la[:], T.am[:], ["am"])
     for b in range(4):
         src = T.b1p[:, C * b:C * (b + 1)].indirect(T.joff[:, 0:3])
         (cp if b < 2 else act)(T.b1t[:, b:4 * K:4], src, ["b1p%d" % b, "joff"], ["b1t%d" % b])
-    quant("b1", T.b1t[:], 128, ["b1t0", "b1t1", "b1t2", "b1t3", "b1tp"])
-    send_mx("b1", far, "lb", 128, "b1", K)
+    quant("b1", 0, T.b1t[:], 128, ["b1t0", "b1t1", "b1t2", "b1t3", "b1tp"])
+    send_codes("b1", far, "lb", 128, "b1", 0, K, ["b1"])
+    send_scales("b1", far, "lb", 128, "b1", 0, K, ["b1"])
 
-    diagonals(0.5)
-    act(T.bt[:, 4 * K:512], T.zer[:, 4 * K:512], ["zer"], ["btp"])
-    act(T.xxt[:, 4 * K:512], T.zer[:, 4 * K:512], ["zer"], ["xxtp"])
-    act(T.q64[:], T.qt[:, 0:4 * K], ["qt"], ["q64"], scale=64.0)
-    quant("lb", T.zer[:], 128, ["zer"], key="lbz")
-    quant("v0", T.vt[:], 128, ["vt"])
-    quant("eh", T.et[:], 512, etk)
-    scan(T.gs[:, 0:K], T.k16[:, 0:K], T.la[:], 0.0, A.mult, A.add, ["k16", "la"], ["gs"])
+    diagonal(0.5)
+    fill(T.bt[:, 4 * K:512], 512 - 4 * K, 0.0, [], ["btp"])
+    fill(T.xxt[:, 4 * K:512], 512 - 4 * K, 0.0, [], ["xxtp"])
+    act(T.q64[:], T.qraw[:], ["qraw"], ["q64"], scale=64.0)
+    quant("lb", 0, T.zer[:, 0:512], 128, ["zer"], key="lbz")
+    quant("v0", 0, T.vt[:], 128, ["vt"])
+    for b in range(4):
+        unit("eh", b)
+    scan(T.gs[:, 0:K], T.k16[:], T.la[:], 0.0, A.mult, A.add, ["k16", "la"], ["gs"])
     cp(T.aoff[:, 0:3], T.gs[:, 15:K:16], ["gs"], ["aoff"])
     for b in range(4):
         src, out = T.xp[:, C * b:C * (b + 1)].indirect(T.aoff[:, 0:3]), T.a0h[:, K * b:K * (b + 1)]
@@ -333,19 +408,20 @@ def rank_program(g, core, T, topo):
             ts(out, src, 0.5, None, A.mult, None, ["xp%d" % b, "aoff"], ["a0h%d" % b])
         else:
             act(out, src, ["xp%d" % b, "aoff"], ["a0h%d" % b], scale=0.5)
-    act(T.arep[:], T.ramp[:].indirect(T.aoff[:, 0:3]), ["ramp", "aoff"], ["arep"])
+    act(T.arep[:], T.ramp[:, 0:C].indirect(T.aoff[:, 0:3]), ["ramp", "aoff"], ["arep"])
     dma("s", "ol", T.ol[:], T.arep[0:128:16, :], r=["arep"])
     for b in range(4):
-        mm(b, "eh", 128 * b, "lb", K, 128, True, True, ["eh", "lb", "lbz"])
+        mm(b, "eh", 128 * b, "lb", K, 128, True, True, ["eh%d" % b, "lb", "lbz"])
     for b in range(4):
         tt(T.bt[:, b:4 * K:4], T["pb%d" % b][:, 128 - K:128], T.a0h[:, K * b:K * (b + 1)], A.add, ["pb%d" % b, "a0h%d" % b], ["bt%d" % b])
-    quant("bb", T.bt[:], 128, ["bt0", "bt1", "bt2", "bt3", "btp"])
-    for b in range(4):
+    quant("bb", 0, T.bt[:], 128, ["bt0", "bt1", "bt2", "bt3", "btp"])
+    for b in (0, 2, 1, 3):
         mm(4 + b, "lw", 128 * b, "bb", 0, 128, True, True, ["lw", "lw2", "bb"])
-    for b in range(4):
+    for b in (0, 2, 1, 3):
         tt(T.tmp[:, b:4 * K:4], T["pb%d" % (4 + b)][:, 0:K], T.q64[:, b:4 * K:4], A.add, ["pb%d" % (4 + b), "q64"], ["tmp%d" % b])
-    ts(T.xxt[:, 0:4 * K], T.tmp[:], 2.0 ** -6, None, A.mult, None, ["tmp0", "tmp1", "tmp2", "tmp3"], ["xxt"])
-    quant("xx", T.xxt[:], 128, ["xxt", "xxtp"])
+    act(T.xxt[:, 0:4 * K:2], T.tmp[:, 0:4 * K:2], ["tmp0", "tmp2"], ["xxt0"], scale=2.0 ** -6)
+    ts(T.xxt[:, 1:4 * K:2], T.tmp[:, 1:4 * K:2], 2.0 ** -6, None, A.mult, None, ["tmp1", "tmp3"], ["xxt1"])
+    quant("xx", 0, T.xxt[:], 128, ["xxt0", "xxt1", "xxtp"])
     mm(0, "v0", 0, "xx", 0, 128, True, True, ["v0", "xx"])
     dma("s", "oc", T.oc[:], T.xxc[:, 0:K].bitcast(dt.uint8), r=["xx"])
     for k in range(4):

@@ -2,35 +2,37 @@ from concourse.mybir import dt, AluOpType, ActivationFunctionType
 
 C, K = 224, 48
 H = 128
+R = C - H
 BF, F32, I32, U16, U8, MX = "bfloat16", "float32", "int32", "uint16", "uint8", "float8_e4m3fn_x4"
 SCRATCH = {}
 for _n, _w in dict(xt=4 * C, ut=512, zt=512, vt=512, qraw=4 * K, qt=512, et=516, zer=516, f0t=1024, t1t=1024, f1t=1024, t2t=1024,
-                   b1p=4 * C, b1t=512, xp=4 * C, bt=512, xxt=512, a0h=4 * K, q64=4 * K,
+                   b1p=4 * C, st=512, xp=4 * C, a0h=4 * K, q64=4 * K,
                    t16=C, ramp=C + 2, mneg=96, mb=C + 2, db=C + 2, dz=C + 4, c4=C,
-                   ms=96, k16=K, kw=192, kq=192, k225=3 * (C + 1), twos=16,
-                   bit=C + 4, zi=C + 4, bm=C, yy=C, pp=C, oo=C, oex=C + 8, oex2=C + 8, gxa=192, gxb=192, gs=192,
-                   eb=192, etr=192, x1=3 * (C + 1), s1=3 * (C + 1), junk=3 * C,
-                   or1=C, or2=C, am=K, la=K, m0=10, m1s=12, lm0=10, lm1=12).items():
+                   ms=96, own=K, k16=K, kw=192, kq=192, ones=C, twos=16,
+                   bit=C + 4, zi=C + 4, bm=C, yy=C, pp=C, oo=C, oex=C + 8, oex2=C + 8, gxa=192, gs=192,
+                   eb=192, etr=192, x1=3 * C, s1=3 * C, junk=3 * C,
+                   or1=C, or2=C, am=K, m0=10, m1s=12, lm0=10, lm1=12).items():
     SCRATCH[_n] = ("sbuf", [128, _w], BF)
 for _n, _w in dict(pf=24, pw=40, wk=40, th=20, tmp=4 * K, ys=K, arep=K).items():
     SCRATCH[_n] = ("sbuf", [128, _w], F32)
 SCRATCH["pc"] = ("sbuf", [128, 16], I32)
-for _n, _w in dict(uoff=8, poff0=14, poff1=14, lp0=14, lp1=14, off4=56, woff=6, joff=4, aoff=4).items():
+for _n, _w in dict(uoff=8, poff0=14, poff1=14, lp0=14, lp1=14, off4=56, woff=6, joff=4, ljoff=4, aoff=4, laoff=4, xoff=16, ooff=56, looff=56).items():
     SCRATCH[_n] = ("sbuf", [128, _w], U16)
-for _n, _w in dict(lw=512, x0=C, u0=128, up=128, z0=128, q0=128, v0=128, e64=512, eh=512, f0=256, l0=C, t1=256, f1=256, l1=C, t2=256,
-                   b1=128, lb=128 + K, bb=128, xx=128).items():
+for _n, _w in dict(lw=512, x0=256, u0=128, up=128, z0=128, q0=128, v0=128, e64=512, eh=512, f0=256, l0=C, t1=256, f1=256, l1=C + K, t2=256,
+                   b1=128, bb=128, xx=128).items():
     SCRATCH[_n + "c"] = ("sbuf", [128, _w], MX)
     SCRATCH[_n + "s"] = ("sbuf", [128, _w], U8)
 for _b in range(8):
     SCRATCH["pb%d" % _b] = ("psum", [128, 512], F32)
 
-DMAS = ["x", "u", "q", "z", "wc", "ws", "v", "ol", "oc", "os0", "os1", "os2", "os3", "y"]
-ARRIVALS = ["p0", "f0a", "f0b", "m0", "p1", "f1a", "f1b", "m1", "a", "b1"]
+DMAS = ["x", "x2", "u", "q", "z", "wc", "ws", "v", "ol", "oc", "os0", "os1", "os2", "os3", "y"]
+ARRIVALS = ["p0", "f0a", "f0b", "m0", "p1", "f1a", "f1b", "m1", "o", "j", "a", "b1"]
 SEMAPHORES = ["cg", "cv", "ca", "cp", "sent"] + ["d_" + n for n in DMAS] + ["r_" + n for n in ARRIVALS]
 
 A = AluOpType
 ACT = ActivationFunctionType
 BIG = 255.0
+STEEP = 64.0
 MID = C / 2
 
 
@@ -123,11 +125,23 @@ def rank_program(g, core, T, topo):
     def fill(out, cols, c, r, w):
         act(out, T.zer[:, 0:cols], ["zer"] + r, w, bias=c)
 
-    def iota(out, pattern, cm, w, small=True):
+    def pad(t, a, b):
+        fill(T[t][:, a:b], b - a, 0.0, [], [t + "p"])
+
+    def pads(t):
+        pad(t, 4 * C, 8 * H)
+
+    def iota(out, pattern, cm, w, small=True, base=0):
         if small:
-            op("g", lambda: g.iota(out, pattern, 0, cm, allow_small_or_imprecise_dtypes=True), (), w)
+            op("g", lambda: g.iota(out, pattern, base, cm, allow_small_or_imprecise_dtypes=True), (), w)
         else:
-            op("g", lambda: g.iota(out, pattern, 0, cm), (), w)
+            op("g", lambda: g.iota(out, pattern, base, cm), (), w)
+
+    def restarts(out, runs, run, w):
+        op("g", lambda: g.affine_select(out, T.ones[:, 0:runs * run], [[0, runs], [1, run]], A.not_equal, 0.0, 0, 0), ["ones"], w)
+
+    def nothing():
+        pass
 
     arrival("p0", far, 1, ["lp0"])
     arrival("f0a", prv, 2, ["l0a"])
@@ -137,23 +151,34 @@ def rank_program(g, core, T, topo):
     arrival("f1a", prv, 2, ["l1a"])
     arrival("f1b", prv, 1, ["l1b"])
     arrival("m1", prv, 1, ["lm1"])
-    arrival("a", far, 1, ["la"])
+    arrival("o", far, 1, ["looff"])
+    arrival("j", far, 1, ["ljoff"])
+    arrival("a", far, 1, ["laoff"])
     arrival("b1", far, 2, ["lb"])
 
     dma("s", "u", T.ut[:], T.u[:], w=["ut"])
-    ms(T.mb[:, C:C + 1], BIG, ["mbe"])
+    ms(T.mb[:, C:C + 1], -BIG, ["mbe"])
     ms(T.zer[:], 0.0, ["zer"])
-    dma("a", "x", T.xt[:], T.x[:], r=["mbe"], w=["xt"])
-    dma("s", "q", T.qraw[:], T.q[:], r=["xt"], w=["qraw"])
-    dma("s", "z", T.zt[:], T.z[:], w=["zt"])
+    dma("a", "x", T.xt[:, 0:4 * H], T.x[:, 0:4 * H], r=["mbe"], w=["xta"])
+    dma("a", "x2", T.xt[:, 4 * H:4 * C], T.x[:, 4 * H:4 * C], w=["xt"])
+    dma("a", "q", T.qraw[:], T.q[:], w=["qraw"])
+    dma("s", "z", T.zt[:], T.z[:], r=["ut"], w=["zt"])
     dma("s", "wc", T.lwc[:].bitcast(dt.uint8), T.wc[:], w=["lw"])
     dma("s", "ws", T.lws[:], T.ws[:], w=["lw2"])
 
-    pc, pf = T.pc, T.pf
+    pc, pf, W = T.pc, T.pf, T.wk
     iota(pc[:, 0:2], [[12, 2]], 1, ["pc0"], small=False)
-    iota(T.ramp[:], [[1, C + 2]], 0, ["ramp"])
     iota(pc[:, 8:16], [[16, 8]], 0, ["u16i"], small=False)
+    iota(T.ramp[:], [[1, C + 2]], 0, ["ramp"])
     iota(T.t16[:], [[0, C // 16], [1, 16]], 0, ["t16"])
+    iota(T.bit[:, C:C + 3], [[-1, 3]], 0, ["bite"], base=1)
+    iota(T.dz[:, C + 1:C + 3], [[2 * int(BIG), 2]], 0, ["dze"], base=-int(BIG))
+    iota(T.oex[:, 0:1], [[0, 1]], 0, ["oexe"])
+    iota(T.ones[:], [[0, C]], 0, ["ones"], base=1)
+    iota(T.gxa[:], [[0, 192]], 0, ["gxa0"])
+    restarts(T.kw[:], 6, 32, ["kw"])
+    iota(T.twos[:], [[0, 16]], 0, ["twos"], base=2)
+    restarts(T.k16[:], 3, 16, ["k16"])
 
     def diagonal(c):
         ts(T.et[:, 3:515:4], T.ramp[:, 0:128], pf[:, 0:1], c, A.is_equal, A.mult, ["ramp", "pf", "et0"], ["et"])
@@ -162,134 +187,146 @@ def rank_program(g, core, T, topo):
         quant(name, 128 * b, T.et[:, 3 - b:515 - b], 128, ["et", "et0"], key=name + str(b))
 
     act(T.et[:], T.zer[:], ["zer"], ["et0"])
-    fill(T.bit[:, C:C + 1], 1, 1.0, [], ["bite"])
-    fill(T.bit[:, C + 1:C + 3], 2, 0.0, [], ["bitf"])
-    fill(T.dz[:, C + 1:C + 2], 1, -BIG, [], ["dze"])
-    fill(T.dz[:, C + 2:C + 3], 1, BIG + 1, [], ["dzf"])
     ts(pc[:, 2:4], pc[:, 0:2], 2, 3, A.logical_shift_right, A.bitwise_and, ["pc0"], ["pc2"])
     ts(pc[:, 4:5], pc[:, 0:1], 15, None, A.bitwise_and, None, ["pc0"], ["pc4"])
-    ts(pc[:, 5:6], pc[:, 0:1], 3, None, A.bitwise_and, None, ["pc0"], ["pc5"])
-    ts(pc[:, 6:7], pc[:, 0:1], 4, 1, A.logical_shift_right, A.bitwise_and, ["pc0"], ["pc6"])
-    ms(T.twos[:], 2.0, ["twos"])
-    cp(pf[:, 0:7], pc[:, 0:7], ["pc0", "pc2", "pc4", "pc5", "pc6"], ["pf"])
-    scan(T.pw[:, 0:16], T.twos[:], T.zer[:, 0:16], 0.5, A.mult, A.add, ["twos", "zer"], ["pw"])
-    ts(pf[:, 7:8], pf[:, 2:3], 0.0, 1024.0, A.is_equal, A.mult, ["pf"], ["s4a"])
-    ts(T.pw[:, 16:32], T.ramp[:, 0:16], pf[:, 4:5], -1.0, A.is_equal, A.mult, ["ramp", "pf"], ["own16"])
-    act(pf[:, 9:10], pf[:, 5:6], ["pf"], ["o4"], bias=-4.0)
-    act(pf[:, 10:11], pf[:, 6:7], ["pf"], ["c16"], scale=-2.0 ** 30, bias=2.0 ** 30)
-    act(pf[:, 11:12], pf[:, 6:7], ["pf"], ["sq"], scale=-1.0, bias=-2.0 ** -30)
+    ts(pc[:, 5:6], pc[:, 0:1], 4, 1, A.logical_shift_right, A.bitwise_and, ["pc0"], ["pc5"])
+    cp(T.uoff[:], pc[:, 8:16], ["u16i"], ["uoff"])
+    cp(pf[:, 0:6], pc[:, 0:6], ["pc0", "pc2", "pc4", "pc5"], ["pf"])
+    op("a", lambda: S.activation(pf[:, 7:8], pf[:, 2:3], ACT.Relu, bias=1024.0, scale=-1024.0), ["pf"], ["s4a"])
+    act(pf[:, 6:7], pf[:, 2:3], ["pf"], ["t4"], scale=-4.0, bias=pf[:, 4:5])
+    act(pf[:, 9:10], pf[:, 6:7], ["t4"], ["o4"], bias=-4.0)
     ts(pf[:, 12:16], T.ramp[:, 0:4], pf[:, 2:3], 256.0, A.is_equal, A.mult, ["ramp", "pf"], ["c4a"])
     ts(pf[:, 16:20], T.ramp[:, 0:4], pf[:, 3:4], 2.0 ** -16, A.not_equal, A.max, ["ramp", "pf"], ["c4b"])
     diagonal(64.0)
-    cp(T.uoff[:], pc[:, 8:16], ["u16i"], ["uoff"])
     tt(pf[:, 20:24], pf[:, 12:16], pf[:, 16:20], A.max, ["c4a", "c4b"], ["c4c"])
-    ts(pf[:, 8:9], pf[:, 7:8], 2.0 ** -6, None, A.max, None, ["s4a"], ["s4"])
-    tt(T.pw[:, 16:32], T.pw[:, 16:32], T.pw[:, 0:16], A.mult, ["pw", "own16"], ["pwm"])
-    for t in range(4):
-        fill(T.c4[:, t:C:4], C // 4, pf[:, 20 + t:21 + t], ["c4c"], ["c4%d" % t])
+    act(pf[:, 8:9], pf[:, 7:8], ["s4a"], ["s4"], bias=2.0 ** -6)
     unit("e64", 0)
-    unit("e64", 1)
-    ts(T.mb[:, 0:C], T.t16[:], pf[:, 4:5], BIG, A.is_equal, A.mult, ["t16", "pf"], ["mb"])
+    ts(T.mb[:, 0:C], T.t16[:], pf[:, 4:5], -BIG, A.is_equal, A.mult, ["t16", "pf"], ["mb"])
 
     quant("u0", 0, T.ut[:], 128, ["ut"])
-    scan(T.db[:, 0:C + 1], T.mb[:, 0:C + 1], T.mb[:, 0:C + 1], 0.0, A.subtract, A.min, ["mb", "mbe"], ["db"])
+    scan(T.db[:, 0:C + 1], T.mb[:, 0:C + 1], T.mb[:, 0:C + 1], 0.0, A.subtract, A.max, ["mb", "mbe"], ["ndb"])
     op("v", lambda: V.tensor_copy(T.upc[:].bitcast(dt.uint32), T.u0c[:].bitcast(dt.uint32).indirect(T.uoff[:, 0:8])), ["u0", "uoff"], ["upa"])
     op("a", lambda: S.activation(T.ups[:], T.u0s[:].indirect(T.uoff[:, 0:8]), ACT.Copy), ["u0", "uoff"], ["upb"])
-    quant("x0", 0, T.xt[:], C, ["xt"])
-    mm(0, "up", 0, "x0", 0, C, True, True, ["upa", "upb", "x0"])
-    ts(T.dz[:, 0:C + 1], T.db[:, 0:C + 1], -1.0, 1.0, A.mult, A.add, ["db"], ["dz"])
-    unit("e64", 2)
-    ts(T.bit[:, 0:C], T.pb0[:, 0:C], 0.0, None, A.is_gt, None, ["pb0"], ["bita", "bitb"])
+    act(T.dz[:, 0:C + 1], T.db[:, 0:C + 1], ["ndb"], ["dz"], bias=1.0)
+    quant("x0", 0, T.xt[:, 0:4 * H], H, ["xta"], key="x0a")
+    mm(0, "up", 0, "x0", 0, H, True, True, ["upa", "upb", "x0a"])
+    quant("x0", H, T.xt[:, 4 * R:4 * C], H, ["xta", "xt"], key="x0b")
+    mm(1, "up", 0, "x0", H, H, True, True, ["upa", "upb", "x0b"])
+    ts(T.bit[:, 0:H], T.pb0[:, 0:H], 0.0, None, A.is_gt, None, ["pb0"], ["bita"])
+    ts(T.bit[:, H:C], T.pb1[:, 2 * H - C:H], 0.0, None, A.is_gt, None, ["pb1"], ["bitb"])
 
-    def order(tile, tkeys, poff, pdst, ftile, fq):
+    def lift(src, a, b, w):
+        scan(T.yy[:, a:b], T[src][:, a:b], T.c4[:, a:b], 0.0, A.max, A.mult, [src, "c40", "c41", "c42", "c43"], w)
+
+    def offsets(off, a, b, r, w):
+        ts(T[off][:, a // 4:b // 4], T.yy[:, a + 3:b:4], pf[:, 8:9], pf[:, 9:10], A.mult, A.add, r + ["s4", "o4"], w)
+
+    def behind(level, a, b):
+        src, r = (T.ramp[:, 16 * a + 1:16 * b + 1], "ramp") if level == 1 else (T.or1[:, 16 * a:16 * b], "or1")
+        cp(T["or%d" % level][:].indirect(T["lp%d" % (level - 1)][:, a:b]), src, [r, "lp%d" % (level - 1)], ["or%d" % level])
+
+    def order(tile, tkeys, poff, pdst, ftile, fq, between):
         bits = ["bita", "bitb"]
-        scan(T.zi[:, 0:C + 3], T.dz[:, 0:C + 3], T.bit[:, 0:C + 3], BIG - 1, A.add, A.subtract, ["dz", "dze", "dzf", "bite", "bitf"] + bits, ["zi"])
-        scan(T.bm[:], T.db[:, 0:C], T.bit[:, 0:C], T.zi[:, C + 1:C + 2], A.add, A.add, ["db", "zi"] + bits, ["bm"])
-        scan(T.yy[:], T.bit[:, 0:C], T.zi[:, 0:C], BIG, A.mult, A.max, ["zi"] + bits, ["yy"])
-        scan(T.pp[:], T.bm[:], T.yy[:], 0.0, A.max, A.min, ["bm", "yy"], ["pp"])
+        scan(T.zi[:, 0:C + 3], T.dz[:, 0:C + 3], T.bit[:, 0:C + 3], BIG - 1, A.add, A.subtract, ["dz", "dze", "bite"] + bits, ["zi"])
+        scan(T.bm[:, ::-1], T.db[:, C:0:-1], T.bit[:, C:0:-1], float(C), A.add, A.subtract, ["ndb", "bite"] + bits, ["bm"])
+        scan(T.yy[:], T.bit[:, 0:C], T.zi[:, 0:C], BIG, A.mult, A.max, ["zi"] + bits, ["yy", "yyb"])
+        scan(T.oex[:, 1:C + 1], T.bit[:, 0:C], T.zer[:, 0:C], 0.0, A.add, A.add, ["zer"] + bits, ["oex"])
+        scan(T.pp[:], T.bm[:], T.yy[:], 0.0, A.max, A.min, ["bm", "yy", "yyb"], ["pp"])
+        between[0]()
         cp(T[poff][:], T.pp[:, 15:C:16], ["pp"], [poff])
+        between[1]()
         send(pdst[0], pdst[1], T["l" + pdst[0]][:], T[poff][:], [poff])
         cp(T.oo[:].indirect(T[poff][:]), T.ramp[:, 1:C + 1], [poff, "ramp"], ["oo"])
-        scan(T.yy[:], T.oo[:], T.c4[:], 0.0, A.max, A.mult, ["oo", "c40", "c41", "c42", "c43"], ["yy"])
-        ts(T.off4[:], T.yy[:, 3:C:4], pf[:, 8:9], pf[:, 9:10], A.mult, A.add, ["yy", "s4", "o4"], ["off4"])
-        win = T[tile][:, 0:4 * C]
-        for eng, a, b, key in ((act, 16, 32, "a1"), (cp, 0, 16, "a0")):
-            eng(T[ftile][:, 16 * a:16 * b], win.indirect(T.off4[:, a:b]), ["off4"] + tkeys, [ftile + key])
-        act(T[ftile][:, 16 * 40:16 * 56], win.indirect(T.off4[:, 40:56]), ["off4"] + tkeys, [ftile + "b1"])
+        between[2]()
+        for a, b, k in ((0, H, ["yy"]), (H, C, ["yyb"])):
+            lift("oo", a, b, k)
+        between[3]()
+        for a, b, k in ((0, H, "yy"), (H, C, "yyb")):
+            offsets("off4", a, b, [k], ["off4" + k])
+
+        def take(eng, a, b, key):
+            eng(T[ftile][:, 16 * a:16 * b], tile.indirect(T.off4[:, a:b]), ["off4yy" if a < H // 4 else "off4yyb"] + tkeys, [ftile + key])
+
+        take(act, 16, 32, "a1")
+        take(cp, 0, 16, "a0")
+        take(act, 38, 56, "b1")
+        between[4]()
         quant(fq, 0, T[ftile][:, 0:4 * H], H, [ftile + "a0", ftile + "a1"], key=fq + "a")
         send_codes(fq + "a", nxt, "l" + fq[1], 0, fq, 0, H, [fq + "a"])
-        cp(T[ftile][:, 16 * 32:16 * 40], win.indirect(T.off4[:, 32:40]), ["off4"] + tkeys, [ftile + "b0"])
+        take(cp, 32, 38, "b0")
+        between[5]()
         quant(fq, H, T[ftile][:, 4 * H:8 * H], H, [ftile + "b0", ftile + "b1", ftile + "p"], key=fq + "b")
         send_scales(fq + "a", nxt, "l" + fq[1], 0, fq, 0, C, [fq + "a", fq + "b"])
-        send_codes(fq + "b", nxt, "l" + fq[1], H, fq, H, C - H, [fq + "b"])
+        send_codes(fq + "b", nxt, "l" + fq[1], H, fq, H, R, [fq + "b"])
 
-    for t in ("f0t", "t1t"):
-        fill(T[t][:, 4 * C:8 * H], 8 * H - 4 * C, 0.0, [], [t + "p"])
-    fill(T.qt[:, 8 * K:512], 512 - 8 * K, 0.0, [], ["qtp"])
-    fill(T.k225[:, 0:338], 338, 1.0, [], ["k225a"])
-    fill(T.k225[:, 338:675], 337, 1.0, [], ["k225b"])
-    fill(T.oex[:, 0:1], 1, 0.0, [], ["oexe"])
-    fill(T.k225[:, 0:675:C + 1], 3, 0.0, ["k225a", "k225b"], ["k225"])
-    fill(T.kw[:], 192, 1.0, [], ["kwa"])
-    fill(T.kq[:], 192, 1.0, [], ["kqa"])
-    fill(T.gxa[:], 192, 0.0, [], ["gxa0"])
-    act(T.mneg[:], T.mb[:, 0:96], ["mb"], ["mneg"], scale=-1.0 / BIG)
-    for a, b, k in ((16, 22, 32), (22, 29, 33)):
-        op("a", lambda a=a, b=b, k=k: S.activation(T.junk[:, a:b], T.pw[:, a:b], ACT.Copy, accum_out=T.pw[:, k:k + 1]), ["pwm"], ["w%d" % k])
+    for t in range(4):
+        fill(T.c4[:, t:C:4], C // 4, pf[:, 20 + t:21 + t], ["c4c"], ["c4%d" % t])
+    act(pf[:, 10:11], pf[:, 5:6], ["pf"], ["c16"], scale=-2.0 ** 30, bias=2.0 ** 30)
+    act(pf[:, 11:12], pf[:, 5:6], ["pf"], ["sq"], scale=-1.0, bias=-2.0 ** -30)
+    pads("f0t")
+    pad("qt", 8 * K, 512)
+    act(T.mneg[:], T.mb[:, 0:96], ["mb"], ["mneg"], scale=1.0 / BIG)
+    act(pf[:, 7:8], pf[:, 11:12], ["sq", "s4"], ["sqk"], scale=2.0 ** -6)
+    act(T.kq[:], T.kw[:], ["kw"], ["kq0"])
+    fill(T.kq[:, 16:192:32], 6, pf[:, 10:11], ["kq0", "c16"], ["kq1"])
     for s in range(6):
         act(T.qt[:, 64 * s:64 * (s + 1)], T.qraw[:, 64 * (s // 2):64 * (s // 2 + 1)], ["qraw"], ["qt%d" % s])
 
-    order("xt", ["xt"], "poff0", ("p0", far), "f0t", "f0")
+    order(T.xt[:], ["xt", "xta"], "poff0", ("p0", far), "f0t", "f0",
+          [nothing, lambda: scan(T.pw[:, 0:16], T.twos[:], T.zer[:, 0:16], 0.5, A.mult, A.add, ["twos", "zer"], ["pw"]),
+           lambda: tt(T.pw[:, 16:32], T.pw[:, 0:16], T.mneg[:, 0:16], A.mult, ["pw", "mneg"], ["pwm"]), nothing,
+           lambda: quant("z0", 0, T.zt[:], 128, ["zt"]),
+           lambda: quant("q0", 0, T.qt[:], 128, ["qtp"] + ["qt%d" % s for s in range(6)])])
 
-    quant("q0", 0, T.qt[:], 128, ["qtp"] + ["qt%d" % s for s in range(6)])
-    quant("z0", 0, T.zt[:], 128, ["zt"])
+    for a, b, k in ((16, 22, 32), (22, 29, 33)):
+        op("a", lambda a=a, b=b, k=k: S.activation(T.junk[:, a:b], T.pw[:, a:b], ACT.Copy, accum_out=T.pw[:, k:k + 1]), ["pwm"], ["w%d" % k])
     mm(7, "z0", 0, "q0", 0, 128, True, True, ["z0", "q0"])
-    unit("e64", 3)
-    fill(T.kw[:, 0:192:32], 6, 0.0, ["kwa"], ["kw"])
-    fill(T.kq[:, 0:192:32], 6, 0.0, ["kqa"], ["kq0"])
-    fill(T.kq[:, 16:192:32], 6, pf[:, 10:11], ["kqa", "c16"], ["kq1"])
-    scan(T.oex[:, 1:C + 1], T.k225[:, 1:C + 1], T.bit[:, 0:C], 0.0, A.mult, A.add, ["k225", "bita", "bitb"], ["oex"])
+    for b in range(1, 4):
+        unit("e64", b)
+    pads("t1t")
     for k in range(2):
         ts(T.eb[:, 96 * k:96 * (k + 1)], T.pb7[:, 0:96], 0.0, T.pw[:, 32 + k:33 + k], A.is_gt, A.mult, ["pb7", "w%d" % (32 + k)], ["eb%d" % k])
     op("v", lambda: V.transpose(T.etr[:], T.eb[:]), ["eb0", "eb1"], ["etr"])
+    behind(1, 0, 4)
     scan(T.eb[:], T.kq[:], T.etr[:], 0.0, A.mult, A.add, ["kq0", "kq1", "etr"], ["eb0", "eb1"])
-    W = T.wk
+    behind(1, 4, 8)
     for k in range(2):
         ts(T.woff[:, 3 * k:3 * k + 3], T.eb[:, 31:96:32], pf[:, 11:12], 128.0 * k, A.mult, A.add, ["eb0", "sq"], ["woff%d" % k])
     for k in range(2):
-        ts(T.gxa[:, 96 * k + 31:96 * (k + 1):32], T.eb[:, 31:96:32], pf[:, 11:12], 128.0 * k, A.mult, A.add, ["eb0", "sq", "gxa0"], ["gxs%d" % k])
-    ts(W[:, 33:36], T.eb[:, 127:192:32], pf[:, 11:12], 2.0 ** -6, A.mult, A.mult, ["eb0", "sq"], ["k0"])
+        act(T.gxa[:, 96 * k + 31:96 * (k + 1):32], T.eb[:, 31:96:32], ["eb0", "sq", "gxa0"], ["gxs%d" % k], scale=pf[:, 11:12], bias=128.0 * k)
+    act(W[:, 33:36], T.eb[:, 127:192:32], ["eb0", "sqk"], ["k0"], scale=pf[:, 7:8])
 
     def walk(kk, kkey, out, okey):
         x0, gs = T.gs[:, 31:192:32], T.gs
         yield tt(T.gxa[:, 0:192:2], T.oex[:, 0:C + 1].indirect(T.woff[:]), T.mneg[:], A.mult, ["oex", "oexe", "woff0", "woff1", "mneg", "gxa0"], ["gxa"])
-        yield scan(gs[:], T.kw[:], T.gxa[:], 0.0, A.mult, A.add, ["kw", "gxa", "gxs0", "gxs1"], ["gs"])
-        tt(W[:, 12:15], gs[:, 127:192:32], gs[:, 31:96:32], A.subtract, ["gs"], ["wn"])
+        yield scan(gs[:], T.kw[:], T.gxa[:], 0.0, A.mult, A.add, ["kw", "gxa", "gxs0", "gxs1", "gxs2"], ["gs"])
+        yield tt(W[:, 12:15], gs[:, 127:192:32], gs[:, 31:96:32], A.subtract, ["gs"], ["wn"])
         yield ts(W[:, 6:12], gs[:, 30:192:32], -1.0, T.zi[:, C + 2:C + 3], A.mult, A.add, ["gs", "zi"], ["w1"])
-        tt(W[:, 16:19], kk, W[:, 12:15], A.is_ge, [kkey, "wn"], ["wc0"])
-        tt(W[:, 19:22], kk, W[:, 12:15], A.is_ge, [kkey, "wn"], ["wc1"])
+        yield tt(W[:, 16:19], kk, W[:, 12:15], A.is_ge, [kkey, "wn"], ["wc0"])
+        yield tt(W[:, 19:22], kk, W[:, 12:15], A.is_ge, [kkey, "wn"], ["wc1"])
         yield tt(W[:, 24:30], W[:, 6:12], x0, A.subtract, ["gs", "w1"], ["wd"])
-        tt(W[:, 30:33], W[:, 16:19], W[:, 12:15], A.mult, ["wc0", "wn"], ["wcz"])
+        yield tt(W[:, 30:33], W[:, 16:19], W[:, 12:15], A.mult, ["wc0", "wn"], ["wcz"])
         yield tt(W[:, 0:6], W[:, 24:30], W[:, 16:22], A.mult, ["wd", "wc0", "wc1"], ["we"])
-        tt(out[:, 6:9], kk, W[:, 30:33], A.subtract, [kkey, "wcz"], [okey + "k"])
+        yield tt(out[:, 6:9], kk, W[:, 30:33], A.subtract, [kkey, "wcz"], [okey + "k"])
         yield tt(out[:, 0:6], W[:, 0:6], x0, A.add, ["gs", "we"], [okey + "l"])
 
     def steps(it, k):
         for _ in range(k):
-            next(it, None)
+            next(it)
 
     def products(land, half):
-        c0, r = ((0, [land + "a"]), (C - H, [land + "a", land + "b"]))[half]
+        c0, r = ((0, [land + "a"]), (R, [land + "a", land + "b"]))[half]
         for b in range(4):
             mm(4 * half + b, "lw", 128 * b, land, c0, H, True, False, ["lw", "lw2"] + r)
             mm(4 * half + b, "e64", 128 * b, land, c0, H, False, True, ["e64%d" % b] + r)
 
-    def casts(tile, half):
-        a, b0, c0 = ((0, 4 * H, 0), (4 * H, 4 * C, 2 * H - C))[half]
-        for b in range(4):
-            pb = "pb%d" % (4 * half + b)
-            act(T[tile][:, a + b:b0:4], T[pb][:, c0:H], [pb], [tile + str(4 * half + b)], scale=2.0 ** -6)
-        return [tile + str(4 * half + b) for b in range(4)]
+    def layer(land, tile):
+        products(land, 0)
+        products(land, 1)
+        for bank in range(8):
+            a, b0, c0 = ((0, 4 * H, 0), (4 * H, 4 * C, H - R))[bank // 4]
+            act(T[tile][:, a + bank % 4:b0:4], T["pb%d" % bank][:, c0:H], ["pb%d" % bank], [tile + str(bank)], scale=2.0 ** -6)
+        return [tile + str(b) for b in range(4)], [tile + str(b) for b in range(4, 8)]
 
     def scores(tq, half):
         mm(half, "up", 0, tq, H * half, H, True, True, ["upa", "upb", tq + "ab"[half]])
@@ -299,129 +336,139 @@ def rank_program(g, core, T, topo):
         ts(T.bit[:, a:b], T["pb%d" % half][:, 0:b - a], 0.0, None, A.is_gt, None, ["pb%d" % half], ["bit" + "ab"[half]])
 
     w0 = walk(W[:, 33:36], "k0", T.m0, "m0")
+    for a, b in ((8, 12), (12, 14)):
+        steps(w0, 1)
+        behind(1, a, b)
     steps(w0, 2)
-    cp(T.or1[:].indirect(T.lp0[:]), T.ramp[:, 0:C], ["lp0", "ramp"], ["or1"])
     dma("s", "v", T.vt[:], T.v[:], r=["l0b"], w=["vt"])
 
-    products("l0", 0)
-    ka = casts("t1t", 0)
-    products("l0", 1)
-    kb = casts("t1t", 1)
+    ka, kb = layer("l0", "t1t")
     quant("t1", 0, T.t1t[:, 0:4 * H], H, ka, key="t1a")
     scores("t1", 0)
-    steps(w0, 2)
+    steps(w0, 3)
     quant("t1", H, T.t1t[:, 4 * H:8 * H], H, kb + ["t1tp"], key="t1b")
     scores("t1", 1)
     steps(w0, 1)
     bits(0)
-    steps(w0, 1)
-    send("m0", nxt, T.lm0[:, 0:9], T.m0[:, 0:9], ["m0k", "m0l"])
     bits(1)
-    for t in ("f1t", "t2t"):
-        fill(T[t][:, 4 * C:8 * H], 8 * H - 4 * C, 0.0, [], [t + "p"])
-    fill(T.gxb[:], 192, 0.0, [], ["gxb0"])
-    fill(T.gxb[:, 1:96:32], 3, -MID, ["gxb0"], ["gxb1"])
-    fill(T.gxb[:, 97:192:32], 3, 0.5, ["gxb0"], ["gxb2"])
+    steps(w0, 1)
+    pads("f1t")
+    pads("t2t")
+    op("a", lambda: S.activation(T.own[:], T.mb[:, 0:K], ACT.Sigmoid, bias=-BIG / 2, scale=-1.0), ["mb"], ["own"])
     fill(T.oex2[:, 0:1], 1, -MID, [], ["oex2e"])
-    act(T.ms[:, 0:K], T.mneg[:, 0:K], ["mneg"], ["msa"])
-    act(T.ms[:, K:96], T.mneg[:, 0:K], ["mneg"], ["msb"], scale=-1.0)
-    order("t1t", ka + kb, "poff1", ("p1", nxt), "f1t", "f1")
-    scan(T.oex[:, 1:C + 1], T.k225[:, 1:C + 1], T.bit[:, 0:C], 0.0, A.mult, A.add, ["k225", "bita", "bitb"], ["oex"])
-    cp(T.woff[:], T.lm0[:, 0:6], ["lm0"], ["woff0", "woff1"])
-    cp(T.gxa[:, 31:192:32], T.lm0[:, 0:6], ["lm0"], ["gxs0", "gxs1"])
+    act(T.ms[:, 0:K], T.mneg[:, 0:K], ["mneg"], ["msa"], scale=STEEP)
+    act(T.ms[:, K:96], T.mneg[:, 0:K], ["mneg"], ["msb"], scale=-STEEP)
+
+    def walked():
+        steps(w0, 1)
+        send("m0", nxt, T.lm0[:, 0:9], T.m0[:, 0:9], ["m0k", "m0l"])
+
+    order(T.t1t[:, 0:4 * C], ka + kb, "poff1", ("p1", nxt), "f1t", "f1",
+          [lambda: steps(w0, 1), walked, nothing, nothing, nothing,
+           lambda: cp(T.woff[:], T.lm0[:, 0:6], ["lm0"], ["woff0", "woff1"])])
+    act(T.gxa[:, 31:192:32], T.lm0[:, 0:6], ["lm0"], ["gxs0", "gxs1"])
     w1 = walk(T.lm0[:, 6:9], "lm0", T.m1s, "m1")
-    steps(w1, 6)
+    for a, k in ((0, 1), (2, 1), (4, 9)):
+        steps(w1, k)
+        behind(2, a, a + 2)
     tt(W[:, 33:36], T.m1s[:, 0:3], T.m1s[:, 6:9], A.add, ["m1k", "m1l"], ["wlk"])
+    behind(2, 6, 8)
     ts(T.m1s[:, 6:9], W[:, 33:36], 0.5 - MID, None, A.add, None, ["wlk"], ["m1k"])
     tt(T.m1s[:, 9:12], W[:, 33:36], T.m1s[:, 3:6], A.subtract, ["wlk", "m1l"], ["m1w"])
     send("m1", nxt, T.lm1[:], T.m1s[:], ["m1k", "m1l", "m1w"])
-    fill(T.x1[:, 0:675:C + 1], 3, -float(C), [], ["x1e"])
-    fill(T.b1t[:, 4 * K:512], 512 - 4 * K, 0.0, [], ["b1tp"])
-    fill(T.k16[:], K, 1.0, [], ["k16a"])
-    fill(T.k16[:, 0:K:16], 3, 0.0, ["k16a"], ["k16"])
-    for b in range(4):
-        act(T.xp[:, C * b:C * (b + 1)], T.xt[:, b:4 * C:4], ["xt"], ["xp%d" % b])
+    pad("st", 4 * K, 512)
+    fill(T.gxa[:, 1:96:32], 3, -MID * STEEP, [], ["gxs0"])
+    fill(T.gxa[:, 97:192:32], 3, 0.5 * STEEP, [], ["gxs1"])
 
-    products("l1", 0)
-    ka = casts("t2t", 0)
-    products("l1", 1)
-    kb = casts("t2t", 1)
-    cp(T.or2[:].indirect(T.lp1[:]), T.or1[:], ["lp1", "or1"], ["or2"])
+    ka, kb = layer("l1", "t2t")
+    behind(2, 8, 14)
     quant("t2", 0, T.t2t[:, 0:4 * H], H, ka, key="t2a")
     scores("t2", 0)
     banks = [2, 3, 4, 5]
-    for b in range(3):
+    for b in range(2):
         mm(banks[b], "e64", 128 * b, "l1", 0, C, True, False, ["e64%d" % b, "l1a", "l1b"])
+    lift("or2", 0, C, ["yy", "yyb"])
+    diagonal(0.5)
+    offsets("ooff", 0, C, ["yy"], ["ooff"])
+    send("o", far, T.looff[:], T.ooff[:], ["ooff"])
     quant("t2", H, T.t2t[:, 4 * H:8 * H], H, kb + ["t2tp"], key="t2b")
     scores("t2", 1)
-    for b in range(3):
+    for b in range(4):
+        if b > 1:
+            mm(banks[b], "e64", 128 * b, "l1", 0, C, True, False, ["e64%d" % b, "l1a", "l1b"])
         mm(banks[b], "e64", 128 * b, "t2", 0, C, False, True, ["e64%d" % b, "t2a", "t2b"])
-    mm(banks[3], "e64", 384, "l1", 0, C, True, False, ["e643", "l1a", "l1b"])
-    mm(banks[3], "e64", 384, "t2", 0, C, False, True, ["e643", "t2a", "t2b"])
 
     def halves(b):
         act(T.b1p[:, C * b:C * (b + 1)], T["pb%d" % banks[b]][:, 0:C], ["pb%d" % banks[b]], ["b1p%d" % b], scale=2.0 ** -7)
 
+    act(T.gxa[:, 31:192:32], T.lm1[:, 6:12], ["lm1"], ["gxs2"], scale=STEEP)
     for b in range(3):
         halves(b)
     bits(0)
-    cp(T.woff[:], T.lm1[:, 0:6], ["lm1"], ["woff0", "woff1"])
-    cp(T.gxb[:, 31:192:32], T.lm1[:, 6:12], ["lm1", "gxb0"], ["gxbs"])
+    scan(T.oex2[:, 1:H + 1], T.bit[:, 0:H], T.zer[:, 0:H], -MID, A.add, A.add, ["zer", "bita"], ["oex2a"])
     bits(1)
-    scan(T.oex2[:, 1:C + 1], T.k225[:, 1:C + 1], T.bit[:, 0:C], -MID, A.mult, A.add, ["k225", "bita", "bitb"], ["oex2"])
-    scan(T.zi[:, 0:C], T.k225[:, 1:C + 1], T.bit[:, 0:C], -MID, A.add, A.subtract, ["k225", "bita", "bitb"], ["zi"])
-    tt(T.gxb[:, 0:192:2], T.oex2[:, 0:C + 1].indirect(T.woff[:]), T.ms[:], A.mult, ["oex2", "oex2e", "woff0", "woff1", "msa", "msb", "gxb0"], ["gxb"])
-    scan(T.gs[:], T.kw[:], T.gxb[:], 0.0, A.mult, A.add, ["kw", "gxb", "gxb1", "gxb2", "gxbs"], ["gs"])
+    cp(T.woff[:], T.lm1[:, 0:6], ["lm1"], ["woff0", "woff1"])
+    scan(T.oex2[:, H + 1:C + 1], T.bit[:, H:C], T.zer[:, 0:R], T.oex2[:, H:H + 1], A.add, A.add, ["zer", "oex2a", "bitb"], ["oex2"])
+    tt(T.gxa[:, 0:192:2], T.oex2[:, 0:C + 1].indirect(T.woff[:]), T.ms[:], A.mult, ["oex2", "oex2e", "woff0", "woff1", "msa", "msb"], ["gxa"])
+    scan(T.zi[:, 0:C], T.ones[:], T.bit[:, 0:C], -MID, A.add, A.subtract, ["ones", "bita", "bitb"], ["zi"])
+    scan(T.gs[:], T.kw[:], T.gxa[:], 0.0, A.mult, A.add, ["kw", "gxa", "gxs0", "gxs1", "gxs2"], ["gs"])
     for s in range(3):
-        op("a", lambda s=s: S.activation(T.junk[:, C * s:C * (s + 1)], T.zi[:, 0:C], ACT.Sign, bias=T.gs[:, 32 * s + 31:32 * s + 32], scale=-1.0,
+        op("a", lambda s=s: S.activation(T.junk[:, C * s:C * (s + 1)], T.zi[:, 0:C], ACT.Sigmoid, bias=T.gs[:, 32 * s + 31:32 * s + 32], scale=-STEEP,
                                          accum_out=T.th[:, 16 + s:17 + s]), ["zi", "gs"], ["s0%d" % s])
-        ts(T.x1[:, (C + 1) * s + 1:(C + 1) * (s + 1)], T.oex2[:, 1:C + 1], T.gs[:, 32 * s + 127:32 * s + 128], 2.0, A.is_le, A.mult, ["oex2", "gs"], ["x1%d" % s])
+        if s == 0:
+            tt(T.th[:, 6:9], T.gs[:, 127:192:32], T.gs[:, 30:96:32], A.add, ["gs"], ["dd"])
+        ts(T.x1[:, C * s:C * (s + 1)], T.oex2[:, 1:C + 1], STEEP, T.gs[:, 32 * s + 127:32 * s + 128], A.mult, A.is_le, ["oex2", "gs"], ["x1%d" % s])
     halves(3)
-    tt(T.th[:, 6:9], T.gs[:, 127:192:32], T.gs[:, 30:96:32], A.add, ["gs"], ["dd"])
-    scan(T.s1[:], T.k225[:], T.x1[:], 0.0, A.mult, A.add, ["k225", "x1e", "x10", "x11", "x12"], ["s1"])
-    ts(T.th[:, 9:12], T.th[:, 6:9], MID, -1000.0, A.add, A.mult, ["dd"], ["cap"])
-    tt(T.th[:, 12:15], T.th[:, 16:19], T.th[:, 9:12], A.min, ["cap", "s00", "s01", "s02"], ["low"])
-    tt(T.th[:, 6:9], T.s1[:, C:675:C + 1], T.th[:, 12:15], A.max, ["s1", "low"], ["dd"])
-    ts(T.joff[:, 0:3], T.th[:, 6:9], 0.5, MID, A.mult, A.add, ["dd"], ["joff"])
-    tt(T.am[:], T.or2[:].indirect(T.joff[:, 0:3]), T.ms[:, K:96], A.mult, ["or2", "joff", "msb"], ["am"])
-    send("a", far, T.la[:], T.am[:], ["am"])
+    ts(T.th[:, 9:12], T.th[:, 6:9], -MID * STEEP, 4.0 * C, A.is_lt, A.mult, ["dd"], ["far"])
+    for s in range(3):
+        scan(T.s1[:, C * s:C * (s + 1)], T.x1[:, C * s:C * (s + 1)], T.zer[:, 0:C], 0.0, A.add, A.add, ["zer", "x1%d" % s], ["s1%d" % s])
+    for s in range(3):
+        ts(T.joff[:, s:s + 1], T.s1[:, C * (s + 1) - 1:C * (s + 1)], T.th[:, 9 + s:10 + s], T.th[:, 16 + s:17 + s], A.add, A.min,
+           ["s0%d" % s, "s1%d" % s, "far"], ["joff%d" % s])
+    joff = ["joff0", "joff1", "joff2"]
+    send("j", far, T.ljoff[:, 0:3], T.joff[:, 0:3], joff)
     for b in range(4):
         src = T.b1p[:, C * b:C * (b + 1)].indirect(T.joff[:, 0:3])
-        (cp if b < 2 else act)(T.b1t[:, b:4 * K:4], src, ["b1p%d" % b, "joff"], ["b1t%d" % b])
-    quant("b1", 0, T.b1t[:], 128, ["b1t0", "b1t1", "b1t2", "b1t3", "b1tp"])
-    send_codes("b1", far, "lb", 128, "b1", 0, K, ["b1"])
-    send_scales("b1", far, "lb", 128, "b1", 0, K, ["b1"])
+        (cp if b < 2 else act)(T.st[:, b:4 * K:4], src, ["b1p%d" % b] + joff, ["st%d" % b])
+    small = ["st0", "st1", "st2", "st3", "stp"]
+    quant("b1", 0, T.st[:], 128, small)
+    tt(T.am[:], T.or2[:].indirect(T.joff[:, 0:3]), T.own[:], A.mult, ["or2", "own"] + joff, ["am"])
+    send_codes("b1", far, "l1", C, "b1", 0, K, ["b1"])
+    send_scales("b1", far, "l1", C, "b1", 0, K, ["b1"])
 
-    diagonal(0.5)
-    fill(T.bt[:, 4 * K:512], 512 - 4 * K, 0.0, [], ["btp"])
-    fill(T.xxt[:, 4 * K:512], 512 - 4 * K, 0.0, [], ["xxtp"])
-    act(T.q64[:], T.qraw[:], ["qraw"], ["q64"], scale=64.0)
-    quant("lb", 0, T.zer[:, 0:512], 128, ["zer"], key="lbz")
-    quant("v0", 0, T.vt[:], 128, ["vt"])
-    for b in range(4):
+    act(T.xp[:, 0:16 * 48], T.xt[:].indirect(T.looff[:, 0:48]), ["xt", "xta", "looff"], ["xp0"])
+    scan(T.gs[:, 0:K], T.k16[:], T.am[:], 0.0, A.mult, A.add, ["k16", "am"], ["gs"])
+    unit("eh", 0)
+    ts(T.aoff[:, 0:3], T.gs[:, 15:K:16], -1.0, None, A.add, None, ["gs"], ["aoff"])
+    send("a", far, T.laoff[:, 0:3], T.aoff[:, 0:3], ["aoff"])
+    for b in range(1, 4):
         unit("eh", b)
-    scan(T.gs[:, 0:K], T.k16[:], T.la[:], 0.0, A.mult, A.add, ["k16", "la"], ["gs"])
-    cp(T.aoff[:, 0:3], T.gs[:, 15:K:16], ["gs"], ["aoff"])
+    cp(T.xp[:, 16 * 48:4 * C], T.xt[:].indirect(T.looff[:, 48:56]), ["xt", "xta", "looff"], ["xp1"])
     for b in range(4):
-        src, out = T.xp[:, C * b:C * (b + 1)].indirect(T.aoff[:, 0:3]), T.a0h[:, K * b:K * (b + 1)]
+        ts(T.xoff[:, 4 * b:4 * b + 3], T.ljoff[:, 0:3], 4.0, float(b), A.mult, A.add, ["ljoff"], ["xoff%d" % b])
+    for b in range(4):
+        src, out = T.xp[:].indirect(T.xoff[:, 4 * b:4 * b + 3]), T.a0h[:, K * b:K * (b + 1)]
         if b < 2:
-            ts(out, src, 0.5, None, A.mult, None, ["xp%d" % b, "aoff"], ["a0h%d" % b])
+            ts(out, src, 0.5, None, A.mult, None, ["xp0", "xp1", "xoff%d" % b], ["a0h%d" % b])
         else:
-            act(out, src, ["xp%d" % b, "aoff"], ["a0h%d" % b], scale=0.5)
-    act(T.arep[:], T.ramp[:, 0:C].indirect(T.aoff[:, 0:3]), ["ramp", "aoff"], ["arep"])
+            act(out, src, ["xp0", "xp1", "xoff%d" % b], ["a0h%d" % b], scale=0.5)
+    quant("v0", 0, T.vt[:], 128, ["vt"])
+    act(T.q64[:], T.qraw[:], ["qraw"], ["q64"], scale=64.0)
+    act(T.arep[:], T.ramp[:, 0:C].indirect(T.laoff[:, 0:3]), ["ramp", "laoff"], ["arep"])
     dma("s", "ol", T.ol[:], T.arep[0:128:16, :], r=["arep"])
     for b in range(4):
-        mm(b, "eh", 128 * b, "lb", K, 128, True, True, ["eh%d" % b, "lb", "lbz"])
+        mm(b, "eh", 128 * b, "l1", C + K - H, H, True, True, ["eh%d" % b, "lb", "l1a", "l1b"])
     for b in range(4):
-        tt(T.bt[:, b:4 * K:4], T["pb%d" % b][:, 128 - K:128], T.a0h[:, K * b:K * (b + 1)], A.add, ["pb%d" % b, "a0h%d" % b], ["bt%d" % b])
-    quant("bb", 0, T.bt[:], 128, ["bt0", "bt1", "bt2", "bt3", "btp"])
+        tt(T.st[:, b:4 * K:4], T["pb%d" % b][:, 128 - K:128], T.a0h[:, K * b:K * (b + 1)], A.add, ["pb%d" % b, "a0h%d" % b], ["st%d" % b])
+    quant("bb", 0, T.st[:], 128, small)
     for b in (0, 2, 1, 3):
         mm(4 + b, "lw", 128 * b, "bb", 0, 128, True, True, ["lw", "lw2", "bb"])
     for b in (0, 2, 1, 3):
         tt(T.tmp[:, b:4 * K:4], T["pb%d" % (4 + b)][:, 0:K], T.q64[:, b:4 * K:4], A.add, ["pb%d" % (4 + b), "q64"], ["tmp%d" % b])
-    act(T.xxt[:, 0:4 * K:2], T.tmp[:, 0:4 * K:2], ["tmp0", "tmp2"], ["xxt0"], scale=2.0 ** -6)
-    ts(T.xxt[:, 1:4 * K:2], T.tmp[:, 1:4 * K:2], 2.0 ** -6, None, A.mult, None, ["tmp1", "tmp3"], ["xxt1"])
-    quant("xx", 0, T.xxt[:], 128, ["xxt0", "xxt1", "xxtp"])
+    act(T.st[:, 0:4 * K:2], T.tmp[:, 0:4 * K:2], ["tmp0", "tmp2"], ["st0", "st2"], scale=2.0 ** -6)
+    act(T.st[:, 1:4 * K:4], T.tmp[:, 1:4 * K:4], ["tmp1"], ["st1"], scale=2.0 ** -6)
+    ts(T.st[:, 3:4 * K:4], T.tmp[:, 3:4 * K:4], 2.0 ** -6, None, A.mult, None, ["tmp3"], ["st3"])
+    quant("xx", 0, T.st[:], 128, small)
     mm(0, "v0", 0, "xx", 0, 128, True, True, ["v0", "xx"])
     dma("s", "oc", T.oc[:], T.xxc[:, 0:K].bitcast(dt.uint8), r=["xx"])
     for k in range(4):

from concourse.mybir import dt, AluOpType, ActivationFunctionType

C, K = 224, 48
H = 128
R = C - H
BF, F32, I32, U16, U8, MX = "bfloat16", "float32", "int32", "uint16", "uint8", "float8_e4m3fn_x4"
SCRATCH = {}
for _n, _w in dict(xt=4 * C, ut=512, zt=512, vt=512, qraw=4 * K, qt=512, et=516, zer=516, f0t=1024, t1t=1024, f1t=1024, t2t=1024,
                   b1p=4 * C, st=512, xp=4 * C, a0h=4 * K, q64=4 * K,
                   t16=C, ramp=C + 2, mneg=96, mb=C + 2, db=C + 2, dz=C + 4, c4=C,
                   ms=96, own=K, k16=K, kw=192, kq=192, ones=C, twos=16,
                   bit=C + 4, zi=C + 4, bm=C, yy=C, pp=C, oo=C, oex=C + 8, oex2=C + 8, gxa=192, gs=192,
                   eb=192, etr=192, x1=3 * C, s1=3 * C, junk=3 * C,
                   or1=C, or2=C, am=K, m0=10, m1s=12, lm0=10, lm1=12).items():
    SCRATCH[_n] = ("sbuf", [128, _w], BF)
for _n, _w in dict(pf=24, pw=40, wk=40, th=20, tmp=4 * K, ys=K, arep=K).items():
    SCRATCH[_n] = ("sbuf", [128, _w], F32)
SCRATCH["pc"] = ("sbuf", [128, 16], I32)
for _n, _w in dict(uoff=8, poff0=14, poff1=14, lp0=14, lp1=14, off4=56, woff=6, joff=4, ljoff=4, aoff=4, laoff=4, xoff=16, ooff=56, looff=56).items():
    SCRATCH[_n] = ("sbuf", [128, _w], U16)
for _n, _w in dict(lw=512, x0=256, u0=128, up=128, z0=128, q0=128, v0=128, e64=512, eh=512, f0=256, l0=C, t1=256, f1=256, l1=C + K, t2=256,
                   b1=128, bb=128, xx=128).items():
    SCRATCH[_n + "c"] = ("sbuf", [128, _w], MX)
    SCRATCH[_n + "s"] = ("sbuf", [128, _w], U8)
for _b in range(8):
    SCRATCH["pb%d" % _b] = ("psum", [128, 512], F32)

DMAS = ["x", "x2", "u", "q", "z", "wc", "ws", "v", "ol", "oc", "os0", "os1", "os2", "os3", "y"]
ARRIVALS = ["p0", "f0a", "f0b", "m0", "p1", "f1a", "f1b", "m1", "o", "j", "a", "b1"]
SEMAPHORES = ["cg", "cv", "ca", "cp", "sent"] + ["d_" + n for n in DMAS] + ["r_" + n for n in ARRIVALS]

A = AluOpType
ACT = ActivationFunctionType
BIG = 255.0
STEEP = 64.0
MID = C / 2


def rank_program(g, core, T, topo):
    rank = T.rank_of(core)
    if rank is None:
        return
    n = len(T.cores)
    nxt, far = T.cores[(rank + 1) % n], T.cores[(rank + 2) % n]
    prv = T.cores[(rank - 1) % n]
    Q = {"g": g, "v": g.vector, "a": g.scalar, "p": g.tensor, "s": g.sync}
    V, S, P = g.vector, g.scalar, g.tensor
    ops, writer, readers = [], {}, {}
    sent = [0]

    def op(q, fn, r=(), w=(), sem=None):
        deps = set()
        for k in r:
            if k in writer:
                deps.add(writer[k])
            if k.startswith("pb"):
                deps.update(j for j in readers.get(k, ()) if ops[j]["q"] != q)
        for k in w:
            if k in writer:
                deps.add(writer[k])
            deps.update(readers.get(k, ()))
        i = len(ops)
        ops.append(dict(q=q, fn=fn, deps=deps, sem=sem))
        for k in r:
            readers.setdefault(k, []).append(i)
        for k in w:
            writer[k] = i
            readers[k] = []

    def arrival(name, src, calls, keys):
        for k in keys:
            writer[k] = len(ops)
        ops.append(dict(q=None, deps=set(), sem="r_" + name, arr=calls * len(topo.engines(src, core))))

    def dma(q, name, out, in_, r=(), w=()):
        op(q, lambda: Q[q].dma_start(out, in_), r, w, sem="d_" + name)

    def send(name, dst, out, in_, r):
        rid, pid, _ = topo.addr(dst)
        sent[0] += len(topo.engines(core, dst))
        op("g", lambda: g.remote_dma(out, in_, T.sem["r_" + name], T.sem.sent, pid, rid, topo.mask(core, dst)), r, (), sem="sent")

    def send_codes(name, dst, to, a, frm, b, cols, r):
        send(name, dst, T[to + "c"][:, a:a + cols].bitcast(dt.uint8), T[frm + "c"][:, b:b + cols].bitcast(dt.uint8), r)

    def send_scales(name, dst, to, a, frm, b, cols, r):
        send(name, dst, T[to + "s"][:, a:a + cols], T[frm + "s"][:, b:b + cols], r)

    def quant(name, a, tile, cols, r, key=None):
        op("v", lambda: V.quantize_mx(T[name + "c"][:, a:a + cols], T[name + "s"][:, a:a + cols], tile), r, [key or name])

    def mm(bank, st, a, mv, c0, cols, start, stop, r):
        pb = "pb%d" % bank
        op("p", lambda: P.matmul_mx(T[pb][:, 0:cols], T[st + "c"][:, a:a + 128], T[st + "s"][:, a:a + 128],
                                    T[mv + "c"][:, c0:c0 + cols], T[mv + "s"][:, c0:c0 + cols], start, stop),
           r, [pb] if start else [])
        writer[pb] = len(ops) - 1

    def ts(out, in0, s1, s2, o0, o1, r, w):
        if o1 is None:
            op("v", lambda: V.tensor_scalar(out, in0, s1, None, o0), r, w)
        else:
            op("v", lambda: V.tensor_scalar(out, in0, s1, s2, o0, o1), r, w)

    def tt(out, in0, in1, o, r, w):
        op("v", lambda: V.tensor_tensor(out, in0, in1, o), r, w)

    def cp(out, in_, r, w):
        op("v", lambda: V.tensor_copy(out, in_), r, w)

    def scan(out, d0, d1, init, o0, o1, r, w):
        op("v", lambda: V.tensor_tensor_scan(out, d0, d1, init, o0, o1), r, w)

    def ms(ap, c, w):
        op("v", lambda: V.memset(ap, c), (), w)

    def act(out, in_, r, w, scale=None, bias=None):
        if bias is not None:
            op("a", lambda: S.activation(out, in_, ACT.Identity, bias=bias, scale=1.0 if scale is None else scale), r, w)
        elif scale is not None:
            op("a", lambda: S.activation(out, in_, ACT.Copy, scale=scale), r, w)
        else:
            op("a", lambda: S.activation(out, in_, ACT.Copy), r, w)

    def fill(out, cols, c, r, w):
        act(out, T.zer[:, 0:cols], ["zer"] + r, w, bias=c)

    def pad(t, a, b):
        fill(T[t][:, a:b], b - a, 0.0, [], [t + "p"])

    def pads(t):
        pad(t, 4 * C, 8 * H)

    def iota(out, pattern, cm, w, small=True, base=0):
        if small:
            op("g", lambda: g.iota(out, pattern, base, cm, allow_small_or_imprecise_dtypes=True), (), w)
        else:
            op("g", lambda: g.iota(out, pattern, base, cm), (), w)

    def restarts(out, runs, run, w):
        op("g", lambda: g.affine_select(out, T.ones[:, 0:runs * run], [[0, runs], [1, run]], A.not_equal, 0.0, 0, 0), ["ones"], w)

    def nothing():
        pass

    arrival("p0", far, 1, ["lp0"])
    arrival("f0a", prv, 2, ["l0a"])
    arrival("f0b", prv, 1, ["l0b"])
    arrival("m0", prv, 1, ["lm0"])
    arrival("p1", prv, 1, ["lp1"])
    arrival("f1a", prv, 2, ["l1a"])
    arrival("f1b", prv, 1, ["l1b"])
    arrival("m1", prv, 1, ["lm1"])
    arrival("o", far, 1, ["looff"])
    arrival("j", far, 1, ["ljoff"])
    arrival("a", far, 1, ["laoff"])
    arrival("b1", far, 2, ["lb"])

    dma("s", "u", T.ut[:], T.u[:], w=["ut"])
    ms(T.mb[:, C:C + 1], -BIG, ["mbe"])
    ms(T.zer[:], 0.0, ["zer"])
    dma("a", "x", T.xt[:, 0:4 * H], T.x[:, 0:4 * H], r=["mbe"], w=["xta"])
    dma("a", "x2", T.xt[:, 4 * H:4 * C], T.x[:, 4 * H:4 * C], w=["xt"])
    dma("a", "q", T.qraw[:], T.q[:], w=["qraw"])
    dma("s", "z", T.zt[:], T.z[:], r=["ut"], w=["zt"])
    dma("s", "wc", T.lwc[:].bitcast(dt.uint8), T.wc[:], w=["lw"])
    dma("s", "ws", T.lws[:], T.ws[:], w=["lw2"])

    pc, pf, W = T.pc, T.pf, T.wk
    iota(pc[:, 0:2], [[12, 2]], 1, ["pc0"], small=False)
    iota(pc[:, 8:16], [[16, 8]], 0, ["u16i"], small=False)
    iota(T.ramp[:], [[1, C + 2]], 0, ["ramp"])
    iota(T.t16[:], [[0, C // 16], [1, 16]], 0, ["t16"])
    iota(T.bit[:, C:C + 3], [[-1, 3]], 0, ["bite"], base=1)
    iota(T.dz[:, C + 1:C + 3], [[2 * int(BIG), 2]], 0, ["dze"], base=-int(BIG))
    iota(T.oex[:, 0:1], [[0, 1]], 0, ["oexe"])
    iota(T.ones[:], [[0, C]], 0, ["ones"], base=1)
    iota(T.gxa[:], [[0, 192]], 0, ["gxa0"])
    restarts(T.kw[:], 6, 32, ["kw"])
    iota(T.twos[:], [[0, 16]], 0, ["twos"], base=2)
    restarts(T.k16[:], 3, 16, ["k16"])

    def diagonal(c):
        ts(T.et[:, 3:515:4], T.ramp[:, 0:128], pf[:, 0:1], c, A.is_equal, A.mult, ["ramp", "pf", "et0"], ["et"])

    def unit(name, b):
        quant(name, 128 * b, T.et[:, 3 - b:515 - b], 128, ["et", "et0"], key=name + str(b))

    act(T.et[:], T.zer[:], ["zer"], ["et0"])
    ts(pc[:, 2:4], pc[:, 0:2], 2, 3, A.logical_shift_right, A.bitwise_and, ["pc0"], ["pc2"])
    ts(pc[:, 4:5], pc[:, 0:1], 15, None, A.bitwise_and, None, ["pc0"], ["pc4"])
    ts(pc[:, 5:6], pc[:, 0:1], 4, 1, A.logical_shift_right, A.bitwise_and, ["pc0"], ["pc5"])
    cp(T.uoff[:], pc[:, 8:16], ["u16i"], ["uoff"])
    cp(pf[:, 0:6], pc[:, 0:6], ["pc0", "pc2", "pc4", "pc5"], ["pf"])
    op("a", lambda: S.activation(pf[:, 7:8], pf[:, 2:3], ACT.Relu, bias=1024.0, scale=-1024.0), ["pf"], ["s4a"])
    act(pf[:, 6:7], pf[:, 2:3], ["pf"], ["t4"], scale=-4.0, bias=pf[:, 4:5])
    act(pf[:, 9:10], pf[:, 6:7], ["t4"], ["o4"], bias=-4.0)
    ts(pf[:, 12:16], T.ramp[:, 0:4], pf[:, 2:3], 256.0, A.is_equal, A.mult, ["ramp", "pf"], ["c4a"])
    ts(pf[:, 16:20], T.ramp[:, 0:4], pf[:, 3:4], 2.0 ** -16, A.not_equal, A.max, ["ramp", "pf"], ["c4b"])
    diagonal(64.0)
    tt(pf[:, 20:24], pf[:, 12:16], pf[:, 16:20], A.max, ["c4a", "c4b"], ["c4c"])
    act(pf[:, 8:9], pf[:, 7:8], ["s4a"], ["s4"], bias=2.0 ** -6)
    unit("e64", 0)
    ts(T.mb[:, 0:C], T.t16[:], pf[:, 4:5], -BIG, A.is_equal, A.mult, ["t16", "pf"], ["mb"])

    quant("u0", 0, T.ut[:], 128, ["ut"])
    scan(T.db[:, 0:C + 1], T.mb[:, 0:C + 1], T.mb[:, 0:C + 1], 0.0, A.subtract, A.max, ["mb", "mbe"], ["ndb"])
    op("v", lambda: V.tensor_copy(T.upc[:].bitcast(dt.uint32), T.u0c[:].bitcast(dt.uint32).indirect(T.uoff[:, 0:8])), ["u0", "uoff"], ["upa"])
    op("a", lambda: S.activation(T.ups[:], T.u0s[:].indirect(T.uoff[:, 0:8]), ACT.Copy), ["u0", "uoff"], ["upb"])
    act(T.dz[:, 0:C + 1], T.db[:, 0:C + 1], ["ndb"], ["dz"], bias=1.0)
    quant("x0", 0, T.xt[:, 0:4 * H], H, ["xta"], key="x0a")
    mm(0, "up", 0, "x0", 0, H, True, True, ["upa", "upb", "x0a"])
    quant("x0", H, T.xt[:, 4 * R:4 * C], H, ["xta", "xt"], key="x0b")
    mm(1, "up", 0, "x0", H, H, True, True, ["upa", "upb", "x0b"])
    ts(T.bit[:, 0:H], T.pb0[:, 0:H], 0.0, None, A.is_gt, None, ["pb0"], ["bita"])
    ts(T.bit[:, H:C], T.pb1[:, 2 * H - C:H], 0.0, None, A.is_gt, None, ["pb1"], ["bitb"])

    def lift(src, a, b, w):
        scan(T.yy[:, a:b], T[src][:, a:b], T.c4[:, a:b], 0.0, A.max, A.mult, [src, "c40", "c41", "c42", "c43"], w)

    def offsets(off, a, b, r, w):
        ts(T[off][:, a // 4:b // 4], T.yy[:, a + 3:b:4], pf[:, 8:9], pf[:, 9:10], A.mult, A.add, r + ["s4", "o4"], w)

    def behind(level, a, b):
        src, r = (T.ramp[:, 16 * a + 1:16 * b + 1], "ramp") if level == 1 else (T.or1[:, 16 * a:16 * b], "or1")
        cp(T["or%d" % level][:].indirect(T["lp%d" % (level - 1)][:, a:b]), src, [r, "lp%d" % (level - 1)], ["or%d" % level])

    def order(tile, tkeys, poff, pdst, ftile, fq, between):
        bits = ["bita", "bitb"]
        scan(T.zi[:, 0:C + 3], T.dz[:, 0:C + 3], T.bit[:, 0:C + 3], BIG - 1, A.add, A.subtract, ["dz", "dze", "bite"] + bits, ["zi"])
        scan(T.bm[:, ::-1], T.db[:, C:0:-1], T.bit[:, C:0:-1], float(C), A.add, A.subtract, ["ndb", "bite"] + bits, ["bm"])
        scan(T.yy[:], T.bit[:, 0:C], T.zi[:, 0:C], BIG, A.mult, A.max, ["zi"] + bits, ["yy", "yyb"])
        scan(T.oex[:, 1:C + 1], T.bit[:, 0:C], T.zer[:, 0:C], 0.0, A.add, A.add, ["zer"] + bits, ["oex"])
        scan(T.pp[:], T.bm[:], T.yy[:], 0.0, A.max, A.min, ["bm", "yy", "yyb"], ["pp"])
        between[0]()
        cp(T[poff][:], T.pp[:, 15:C:16], ["pp"], [poff])
        between[1]()
        send(pdst[0], pdst[1], T["l" + pdst[0]][:], T[poff][:], [poff])
        cp(T.oo[:].indirect(T[poff][:]), T.ramp[:, 1:C + 1], [poff, "ramp"], ["oo"])
        between[2]()
        for a, b, k in ((0, H, ["yy"]), (H, C, ["yyb"])):
            lift("oo", a, b, k)
        between[3]()
        for a, b, k in ((0, H, "yy"), (H, C, "yyb")):
            offsets("off4", a, b, [k], ["off4" + k])

        def take(eng, a, b, key):
            eng(T[ftile][:, 16 * a:16 * b], tile.indirect(T.off4[:, a:b]), ["off4yy" if a < H // 4 else "off4yyb"] + tkeys, [ftile + key])

        take(act, 16, 32, "a1")
        take(cp, 0, 16, "a0")
        take(act, 38, 56, "b1")
        between[4]()
        quant(fq, 0, T[ftile][:, 0:4 * H], H, [ftile + "a0", ftile + "a1"], key=fq + "a")
        send_codes(fq + "a", nxt, "l" + fq[1], 0, fq, 0, H, [fq + "a"])
        take(cp, 32, 38, "b0")
        between[5]()
        quant(fq, H, T[ftile][:, 4 * H:8 * H], H, [ftile + "b0", ftile + "b1", ftile + "p"], key=fq + "b")
        send_scales(fq + "a", nxt, "l" + fq[1], 0, fq, 0, C, [fq + "a", fq + "b"])
        send_codes(fq + "b", nxt, "l" + fq[1], H, fq, H, R, [fq + "b"])

    for t in range(4):
        fill(T.c4[:, t:C:4], C // 4, pf[:, 20 + t:21 + t], ["c4c"], ["c4%d" % t])
    act(pf[:, 10:11], pf[:, 5:6], ["pf"], ["c16"], scale=-2.0 ** 30, bias=2.0 ** 30)
    act(pf[:, 11:12], pf[:, 5:6], ["pf"], ["sq"], scale=-1.0, bias=-2.0 ** -30)
    pads("f0t")
    pad("qt", 8 * K, 512)
    act(T.mneg[:], T.mb[:, 0:96], ["mb"], ["mneg"], scale=1.0 / BIG)
    act(pf[:, 7:8], pf[:, 11:12], ["sq", "s4"], ["sqk"], scale=2.0 ** -6)
    act(T.kq[:], T.kw[:], ["kw"], ["kq0"])
    fill(T.kq[:, 16:192:32], 6, pf[:, 10:11], ["kq0", "c16"], ["kq1"])
    for s in range(6):
        act(T.qt[:, 64 * s:64 * (s + 1)], T.qraw[:, 64 * (s // 2):64 * (s // 2 + 1)], ["qraw"], ["qt%d" % s])

    order(T.xt[:], ["xt", "xta"], "poff0", ("p0", far), "f0t", "f0",
          [nothing, lambda: scan(T.pw[:, 0:16], T.twos[:], T.zer[:, 0:16], 0.5, A.mult, A.add, ["twos", "zer"], ["pw"]),
           lambda: tt(T.pw[:, 16:32], T.pw[:, 0:16], T.mneg[:, 0:16], A.mult, ["pw", "mneg"], ["pwm"]), nothing,
           lambda: quant("z0", 0, T.zt[:], 128, ["zt"]),
           lambda: quant("q0", 0, T.qt[:], 128, ["qtp"] + ["qt%d" % s for s in range(6)])])

    for a, b, k in ((16, 22, 32), (22, 29, 33)):
        op("a", lambda a=a, b=b, k=k: S.activation(T.junk[:, a:b], T.pw[:, a:b], ACT.Copy, accum_out=T.pw[:, k:k + 1]), ["pwm"], ["w%d" % k])
    mm(7, "z0", 0, "q0", 0, 128, True, True, ["z0", "q0"])
    for b in range(1, 4):
        unit("e64", b)
    pads("t1t")
    for k in range(2):
        ts(T.eb[:, 96 * k:96 * (k + 1)], T.pb7[:, 0:96], 0.0, T.pw[:, 32 + k:33 + k], A.is_gt, A.mult, ["pb7", "w%d" % (32 + k)], ["eb%d" % k])
    op("v", lambda: V.transpose(T.etr[:], T.eb[:]), ["eb0", "eb1"], ["etr"])
    behind(1, 0, 4)
    scan(T.eb[:], T.kq[:], T.etr[:], 0.0, A.mult, A.add, ["kq0", "kq1", "etr"], ["eb0", "eb1"])
    behind(1, 4, 8)
    for k in range(2):
        ts(T.woff[:, 3 * k:3 * k + 3], T.eb[:, 31:96:32], pf[:, 11:12], 128.0 * k, A.mult, A.add, ["eb0", "sq"], ["woff%d" % k])
    for k in range(2):
        act(T.gxa[:, 96 * k + 31:96 * (k + 1):32], T.eb[:, 31:96:32], ["eb0", "sq", "gxa0"], ["gxs%d" % k], scale=pf[:, 11:12], bias=128.0 * k)
    act(W[:, 33:36], T.eb[:, 127:192:32], ["eb0", "sqk"], ["k0"], scale=pf[:, 7:8])

    def walk(kk, kkey, out, okey):
        x0, gs = T.gs[:, 31:192:32], T.gs
        yield tt(T.gxa[:, 0:192:2], T.oex[:, 0:C + 1].indirect(T.woff[:]), T.mneg[:], A.mult, ["oex", "oexe", "woff0", "woff1", "mneg", "gxa0"], ["gxa"])
        yield scan(gs[:], T.kw[:], T.gxa[:], 0.0, A.mult, A.add, ["kw", "gxa", "gxs0", "gxs1", "gxs2"], ["gs"])
        yield tt(W[:, 12:15], gs[:, 127:192:32], gs[:, 31:96:32], A.subtract, ["gs"], ["wn"])
        yield ts(W[:, 6:12], gs[:, 30:192:32], -1.0, T.zi[:, C + 2:C + 3], A.mult, A.add, ["gs", "zi"], ["w1"])
        yield tt(W[:, 16:19], kk, W[:, 12:15], A.is_ge, [kkey, "wn"], ["wc0"])
        yield tt(W[:, 19:22], kk, W[:, 12:15], A.is_ge, [kkey, "wn"], ["wc1"])
        yield tt(W[:, 24:30], W[:, 6:12], x0, A.subtract, ["gs", "w1"], ["wd"])
        yield tt(W[:, 30:33], W[:, 16:19], W[:, 12:15], A.mult, ["wc0", "wn"], ["wcz"])
        yield tt(W[:, 0:6], W[:, 24:30], W[:, 16:22], A.mult, ["wd", "wc0", "wc1"], ["we"])
        yield tt(out[:, 6:9], kk, W[:, 30:33], A.subtract, [kkey, "wcz"], [okey + "k"])
        yield tt(out[:, 0:6], W[:, 0:6], x0, A.add, ["gs", "we"], [okey + "l"])

    def steps(it, k):
        for _ in range(k):
            next(it)

    def products(land, half):
        c0, r = ((0, [land + "a"]), (R, [land + "a", land + "b"]))[half]
        for b in range(4):
            mm(4 * half + b, "lw", 128 * b, land, c0, H, True, False, ["lw", "lw2"] + r)
            mm(4 * half + b, "e64", 128 * b, land, c0, H, False, True, ["e64%d" % b] + r)

    def layer(land, tile):
        products(land, 0)
        products(land, 1)
        for bank in range(8):
            a, b0, c0 = ((0, 4 * H, 0), (4 * H, 4 * C, H - R))[bank // 4]
            act(T[tile][:, a + bank % 4:b0:4], T["pb%d" % bank][:, c0:H], ["pb%d" % bank], [tile + str(bank)], scale=2.0 ** -6)
        return [tile + str(b) for b in range(4)], [tile + str(b) for b in range(4, 8)]

    def scores(tq, half):
        mm(half, "up", 0, tq, H * half, H, True, True, ["upa", "upb", tq + "ab"[half]])

    def bits(half):
        a, b = ((0, H), (H, C))[half]
        ts(T.bit[:, a:b], T["pb%d" % half][:, 0:b - a], 0.0, None, A.is_gt, None, ["pb%d" % half], ["bit" + "ab"[half]])

    w0 = walk(W[:, 33:36], "k0", T.m0, "m0")
    for a, b in ((8, 12), (12, 14)):
        steps(w0, 1)
        behind(1, a, b)
    steps(w0, 2)
    dma("s", "v", T.vt[:], T.v[:], r=["l0b"], w=["vt"])

    ka, kb = layer("l0", "t1t")
    quant("t1", 0, T.t1t[:, 0:4 * H], H, ka, key="t1a")
    scores("t1", 0)
    steps(w0, 3)
    quant("t1", H, T.t1t[:, 4 * H:8 * H], H, kb + ["t1tp"], key="t1b")
    scores("t1", 1)
    steps(w0, 1)
    bits(0)
    bits(1)
    steps(w0, 1)
    pads("f1t")
    pads("t2t")
    op("a", lambda: S.activation(T.own[:], T.mb[:, 0:K], ACT.Sigmoid, bias=-BIG / 2, scale=-1.0), ["mb"], ["own"])
    fill(T.oex2[:, 0:1], 1, -MID, [], ["oex2e"])
    act(T.ms[:, 0:K], T.mneg[:, 0:K], ["mneg"], ["msa"], scale=STEEP)
    act(T.ms[:, K:96], T.mneg[:, 0:K], ["mneg"], ["msb"], scale=-STEEP)

    def walked():
        steps(w0, 1)
        send("m0", nxt, T.lm0[:, 0:9], T.m0[:, 0:9], ["m0k", "m0l"])

    order(T.t1t[:, 0:4 * C], ka + kb, "poff1", ("p1", nxt), "f1t", "f1",
          [lambda: steps(w0, 1), walked, nothing, nothing, nothing,
           lambda: cp(T.woff[:], T.lm0[:, 0:6], ["lm0"], ["woff0", "woff1"])])
    act(T.gxa[:, 31:192:32], T.lm0[:, 0:6], ["lm0"], ["gxs0", "gxs1"])
    w1 = walk(T.lm0[:, 6:9], "lm0", T.m1s, "m1")
    for a, k in ((0, 1), (2, 1), (4, 9)):
        steps(w1, k)
        behind(2, a, a + 2)
    tt(W[:, 33:36], T.m1s[:, 0:3], T.m1s[:, 6:9], A.add, ["m1k", "m1l"], ["wlk"])
    behind(2, 6, 8)
    ts(T.m1s[:, 6:9], W[:, 33:36], 0.5 - MID, None, A.add, None, ["wlk"], ["m1k"])
    tt(T.m1s[:, 9:12], W[:, 33:36], T.m1s[:, 3:6], A.subtract, ["wlk", "m1l"], ["m1w"])
    send("m1", nxt, T.lm1[:], T.m1s[:], ["m1k", "m1l", "m1w"])
    pad("st", 4 * K, 512)
    fill(T.gxa[:, 1:96:32], 3, -MID * STEEP, [], ["gxs0"])
    fill(T.gxa[:, 97:192:32], 3, 0.5 * STEEP, [], ["gxs1"])

    ka, kb = layer("l1", "t2t")
    behind(2, 8, 14)
    quant("t2", 0, T.t2t[:, 0:4 * H], H, ka, key="t2a")
    scores("t2", 0)
    banks = [2, 3, 4, 5]
    for b in range(2):
        mm(banks[b], "e64", 128 * b, "l1", 0, C, True, False, ["e64%d" % b, "l1a", "l1b"])
    lift("or2", 0, C, ["yy", "yyb"])
    diagonal(0.5)
    offsets("ooff", 0, C, ["yy"], ["ooff"])
    send("o", far, T.looff[:], T.ooff[:], ["ooff"])
    quant("t2", H, T.t2t[:, 4 * H:8 * H], H, kb + ["t2tp"], key="t2b")
    scores("t2", 1)
    for b in range(4):
        if b > 1:
            mm(banks[b], "e64", 128 * b, "l1", 0, C, True, False, ["e64%d" % b, "l1a", "l1b"])
        mm(banks[b], "e64", 128 * b, "t2", 0, C, False, True, ["e64%d" % b, "t2a", "t2b"])

    def halves(b):
        act(T.b1p[:, C * b:C * (b + 1)], T["pb%d" % banks[b]][:, 0:C], ["pb%d" % banks[b]], ["b1p%d" % b], scale=2.0 ** -7)

    act(T.gxa[:, 31:192:32], T.lm1[:, 6:12], ["lm1"], ["gxs2"], scale=STEEP)
    for b in range(3):
        halves(b)
    bits(0)
    scan(T.oex2[:, 1:H + 1], T.bit[:, 0:H], T.zer[:, 0:H], -MID, A.add, A.add, ["zer", "bita"], ["oex2a"])
    bits(1)
    cp(T.woff[:], T.lm1[:, 0:6], ["lm1"], ["woff0", "woff1"])
    scan(T.oex2[:, H + 1:C + 1], T.bit[:, H:C], T.zer[:, 0:R], T.oex2[:, H:H + 1], A.add, A.add, ["zer", "oex2a", "bitb"], ["oex2"])
    tt(T.gxa[:, 0:192:2], T.oex2[:, 0:C + 1].indirect(T.woff[:]), T.ms[:], A.mult, ["oex2", "oex2e", "woff0", "woff1", "msa", "msb"], ["gxa"])
    scan(T.zi[:, 0:C], T.ones[:], T.bit[:, 0:C], -MID, A.add, A.subtract, ["ones", "bita", "bitb"], ["zi"])
    scan(T.gs[:], T.kw[:], T.gxa[:], 0.0, A.mult, A.add, ["kw", "gxa", "gxs0", "gxs1", "gxs2"], ["gs"])
    for s in range(3):
        op("a", lambda s=s: S.activation(T.junk[:, C * s:C * (s + 1)], T.zi[:, 0:C], ACT.Sigmoid, bias=T.gs[:, 32 * s + 31:32 * s + 32], scale=-STEEP,
                                         accum_out=T.th[:, 16 + s:17 + s]), ["zi", "gs"], ["s0%d" % s])
        if s == 0:
            tt(T.th[:, 6:9], T.gs[:, 127:192:32], T.gs[:, 30:96:32], A.add, ["gs"], ["dd"])
        ts(T.x1[:, C * s:C * (s + 1)], T.oex2[:, 1:C + 1], STEEP, T.gs[:, 32 * s + 127:32 * s + 128], A.mult, A.is_le, ["oex2", "gs"], ["x1%d" % s])
    halves(3)
    ts(T.th[:, 9:12], T.th[:, 6:9], -MID * STEEP, 4.0 * C, A.is_lt, A.mult, ["dd"], ["far"])
    for s in range(3):
        scan(T.s1[:, C * s:C * (s + 1)], T.x1[:, C * s:C * (s + 1)], T.zer[:, 0:C], 0.0, A.add, A.add, ["zer", "x1%d" % s], ["s1%d" % s])
    for s in range(3):
        ts(T.joff[:, s:s + 1], T.s1[:, C * (s + 1) - 1:C * (s + 1)], T.th[:, 9 + s:10 + s], T.th[:, 16 + s:17 + s], A.add, A.min,
           ["s0%d" % s, "s1%d" % s, "far"], ["joff%d" % s])
    joff = ["joff0", "joff1", "joff2"]
    send("j", far, T.ljoff[:, 0:3], T.joff[:, 0:3], joff)
    for b in range(4):
        src = T.b1p[:, C * b:C * (b + 1)].indirect(T.joff[:, 0:3])
        (cp if b < 2 else act)(T.st[:, b:4 * K:4], src, ["b1p%d" % b] + joff, ["st%d" % b])
    small = ["st0", "st1", "st2", "st3", "stp"]
    quant("b1", 0, T.st[:], 128, small)
    tt(T.am[:], T.or2[:].indirect(T.joff[:, 0:3]), T.own[:], A.mult, ["or2", "own"] + joff, ["am"])
    send_codes("b1", far, "l1", C, "b1", 0, K, ["b1"])
    send_scales("b1", far, "l1", C, "b1", 0, K, ["b1"])

    act(T.xp[:, 0:16 * 48], T.xt[:].indirect(T.looff[:, 0:48]), ["xt", "xta", "looff"], ["xp0"])
    scan(T.gs[:, 0:K], T.k16[:], T.am[:], 0.0, A.mult, A.add, ["k16", "am"], ["gs"])
    unit("eh", 0)
    ts(T.aoff[:, 0:3], T.gs[:, 15:K:16], -1.0, None, A.add, None, ["gs"], ["aoff"])
    send("a", far, T.laoff[:, 0:3], T.aoff[:, 0:3], ["aoff"])
    for b in range(1, 4):
        unit("eh", b)
    cp(T.xp[:, 16 * 48:4 * C], T.xt[:].indirect(T.looff[:, 48:56]), ["xt", "xta", "looff"], ["xp1"])
    for b in range(4):
        ts(T.xoff[:, 4 * b:4 * b + 3], T.ljoff[:, 0:3], 4.0, float(b), A.mult, A.add, ["ljoff"], ["xoff%d" % b])
    for b in range(4):
        src, out = T.xp[:].indirect(T.xoff[:, 4 * b:4 * b + 3]), T.a0h[:, K * b:K * (b + 1)]
        if b < 2:
            ts(out, src, 0.5, None, A.mult, None, ["xp0", "xp1", "xoff%d" % b], ["a0h%d" % b])
        else:
            act(out, src, ["xp0", "xp1", "xoff%d" % b], ["a0h%d" % b], scale=0.5)
    quant("v0", 0, T.vt[:], 128, ["vt"])
    act(T.q64[:], T.qraw[:], ["qraw"], ["q64"], scale=64.0)
    act(T.arep[:], T.ramp[:, 0:C].indirect(T.laoff[:, 0:3]), ["ramp", "laoff"], ["arep"])
    dma("s", "ol", T.ol[:], T.arep[0:128:16, :], r=["arep"])
    for b in range(4):
        mm(b, "eh", 128 * b, "l1", C + K - H, H, True, True, ["eh%d" % b, "lb", "l1a", "l1b"])
    for b in range(4):
        tt(T.st[:, b:4 * K:4], T["pb%d" % b][:, 128 - K:128], T.a0h[:, K * b:K * (b + 1)], A.add, ["pb%d" % b, "a0h%d" % b], ["st%d" % b])
    quant("bb", 0, T.st[:], 128, small)
    for b in (0, 2, 1, 3):
        mm(4 + b, "lw", 128 * b, "bb", 0, 128, True, True, ["lw", "lw2", "bb"])
    for b in (0, 2, 1, 3):
        tt(T.tmp[:, b:4 * K:4], T["pb%d" % (4 + b)][:, 0:K], T.q64[:, b:4 * K:4], A.add, ["pb%d" % (4 + b), "q64"], ["tmp%d" % b])
    act(T.st[:, 0:4 * K:2], T.tmp[:, 0:4 * K:2], ["tmp0", "tmp2"], ["st0", "st2"], scale=2.0 ** -6)
    act(T.st[:, 1:4 * K:4], T.tmp[:, 1:4 * K:4], ["tmp1"], ["st1"], scale=2.0 ** -6)
    ts(T.st[:, 3:4 * K:4], T.tmp[:, 3:4 * K:4], 2.0 ** -6, None, A.mult, None, ["tmp3"], ["st3"])
    quant("xx", 0, T.st[:], 128, small)
    mm(0, "v0", 0, "xx", 0, 128, True, True, ["v0", "xx"])
    dma("s", "oc", T.oc[:], T.xxc[:, 0:K].bitcast(dt.uint8), r=["xx"])
    for k in range(4):
        dma("s" if k < 2 else "a", "os%d" % k, T.osc[4 * k:4 * k + 4, :], T.xxs[32 * k:32 * k + 4, 0:K], r=["xx"])
    cp(T.ys[:], T.pb0[:, 0:K], ["pb0"], ["ys"])
    dma("a", "y", T.y[:], T.ys[:], r=["ys"])

    needed = set()
    for o in ops:
        needed.update(o["deps"])
    count, token, known = {}, {}, {q: {} for q in Q}
    for i, o in enumerate(ops):
        if o["q"] is None:
            token[i] = (o["sem"], o["arr"], {})
            continue
        q, kn = o["q"], known[o["q"]]
        want = {}
        for d in o["deps"]:
            s, v, _ = token[d]
            want[s] = max(want.get(s, 0), v)
        for d in sorted(o["deps"], reverse=True):
            s, v, clock = token[d]
            if want[s] == v and kn.get(s, 0) < v:
                Q[q].wait_ge(T.sem[s], v)
                kn[s] = v
            for s2, v2 in clock.items():
                if kn.get(s2, 0) < v2:
                    kn[s2] = v2
        ins = o["fn"]()
        if o["sem"] == "sent":
            continue
        if o["sem"]:
            ins.then_inc(T.sem[o["sem"]], 16)
            count[o["sem"]] = 16
            token[i] = (o["sem"], 16, dict(kn))
        elif i in needed:
            s = "c" + q
            ins.then_inc(T.sem[s], 1)
            count[s] = count.get(s, 0) + 1
            token[i] = (s, count[s], dict(kn))
    count["sent"] = sent[0]
    for s in sorted(count, key=lambda s: (s.startswith("d_o") or s == "d_y", s)):
        if not any(known[q].get(s, 0) >= count[s] for q in Q):
            g.wait_ge(T.sem[s], count[s])
